import numpy as np
CORES = [45,53,77,117,47,55,79,119]
N = 8
R, W, T = 4096, 64, 512
CAPP = 128
def entries(a): return a.T.reshape(-1)
def pack(v, P): return np.ascontiguousarray(np.asarray(v, np.int32).reshape(-1, P).T)
def lists(rng, how):
    I = rng.integers(0, N * R, (N, T))
    O = np.stack([rng.permutation(np.repeat(np.arange(N), CAPP))[:T] for r in range(N)])
    if how == "full": O = np.stack([rng.permutation(np.repeat(rng.permutation(N)[:T // CAPP], CAPP)) for r in range(N)])
    I = R * O + rng.integers(0, R, (N, T))
    if how == "alike": I = R * O + rng.integers(0, R, (N, 1))
    if how == "edge": I = R * O + np.where(rng.random((N, T)) < 0.5, 0, R - 1)
    if how == "sorted": I = np.sort(I, axis=1)
    return {"idx": np.stack([pack(I[r], 128) for r in range(N)])}
def setup_inputs(rng):
    return dict({"tab": rng.standard_normal((N, R, W), dtype=np.float32)}, **lists(rng, "uniform"))
def setup_inputs_alike(rng):
    d = setup_inputs(rng); d.update(lists(rng, "alike"))
    for k in ("tab",): d[k] = (d[k].astype(np.float32) * 1048576.0).astype(d[k].dtype)
    return d
def setup_inputs_edge(rng):
    d = setup_inputs(rng); d.update(lists(rng, "edge"))
    for k in ("tab",): d[k] = (d[k].astype(np.float32) * (1 / 1024.0)).astype(d[k].dtype)
    return d
def setup_inputs_full(rng):
    d = setup_inputs(rng); d.update(lists(rng, "full"))
    return d
def setup_inputs_sorted(rng):
    d = setup_inputs(rng); d.update(lists(rng, "sorted"))
    return d
def check_inputs(x):
    bad = []
    if x["idx"].min() < 0 or x["idx"].max() >= N * R: bad.append("idx out of range")
    if max(int(np.bincount(entries(a) // R, minlength=N).max()) for a in x["idx"]) > CAPP: bad.append("more than CAPP entries of a list point into one rank's part")
    return bad
def reference(tab, idx):
    A = np.concatenate(list(tab), axis=0)
    return {"y": np.stack([A[entries(idx[r])] for r in range(N)])}

@@ -1,0 +1,359 @@
+import numpy as np
+from concourse.bass import DstId, RemoteDMATransfer
+from concourse.mybir import dt, AluOpType, AxisListType, ActivationFunctionType
+
+F, I32, B16, U16 = "float32", "int32", "bfloat16", "uint16"
+SCRATCH = {
+    "io8": ("sbuf", [128, 8], F), "ioOZ": ("sbuf", [128, 64], F), "io128": ("sbuf", [128, 128], F),
+    "onesb": ("sbuf", [128, 128], B16), "Lb": ("sbuf", [128, 128], B16),
+    "ones64": ("sbuf", [128, 64], F), "mz1": ("sbuf", [128, 64], F), "mOZ": ("sbuf", [128, 64], F),
+    "Di": ("sbuf", [128, 128], I32), "Da": ("sbuf", [128, 128], I32), "Am": ("sbuf", [128, 128], F),
+    "Ds": ("sbuf", [128, 32], I32), "S4": ("sbuf", [128, 32], F),
+    "pi": ("sbuf", [128, 1], I32), "pa": ("sbuf", [128, 1], I32),
+    "cmO": ("sbuf", [128, 1], F), "cmF": ("sbuf", [128, 1], F),
+    "ix": ("sbuf", [128, 4], I32), "oi": ("sbuf", [128, 4], I32), "ti": ("sbuf", [128, 4], I32),
+    "ki": ("sbuf", [128, 4], I32), "a1": ("sbuf", [128, 4], I32),
+    "of": ("sbuf", [128, 4], F), "v1": ("sbuf", [128, 4], F), "v2": ("sbuf", [128, 4], F),
+    "kf": ("sbuf", [128, 4], F), "v3": ("sbuf", [128, 4], F), "val": ("sbuf", [128, 4], F),
+    "Hp": ("sbuf", [128, 56], B16), "Rv": ("sbuf", [128, 256], F), "tmpS": ("sbuf", [128, 32], F),
+    "slot": ("sbuf", [128, 4], F), "E": ("sbuf", [128, 512], F), "reqS": ("sbuf", [128, 64], F),
+    "tabS": ("sbuf", [128, 2048], F), "winT": ("sbuf", [128, 2176], F), "reqL": ("sbuf", [128, 64], F),
+    "t1": ("sbuf", [128, 64], F), "off1": ("sbuf", [128, 64], U16), "G": ("sbuf", [128, 2048], F),
+    "respS": ("sbuf", [128, 512], F),
+    "land": ("sbuf", [128, 512], F), "LT": ("sbuf", [128, 640], F),
+    "sli": ("sbuf", [128, 4], I32), "hii": ("sbuf", [128, 4], I32), "o64": ("sbuf", [128, 4], F),
+    "w2": ("sbuf", [128, 4], F), "hif": ("sbuf", [128, 4], F), "val2": ("sbuf", [128, 4], F),
+    "B2": ("sbuf", [128, 32], F), "t2": ("sbuf", [128, 32], F), "off2": ("sbuf", [128, 32], U16),
+    "G2": ("sbuf", [128, 1024], F), "Ysb": ("sbuf", [128, 256], F),
+    "hq": ("sbuf", [128, 64], F), "hr": ("sbuf", [128, 256], F),
+    "psS": ("psum", [128, 512], F), "psC": ("psum", [128, 512], F), "psF": ("psum", [128, 512], F),
+    "psY": ("psum", [128, 512], F), "psG0": ("psum", [128, 512], F), "psG1": ("psum", [128, 512], F),
+    "psG2": ("psum", [128, 512], F),
+}
+SEMAPHORES = ["vq", "pq", "aq", "gq", "dix", "dtab", "dy", "rq0", "rq1", "rq2", "rs", "hqs", "hr1", "hr2", "loc"]
+
+
+def _bits(mask):
+    return [b for b in range(16) if (mask >> b) & 1]
+
+
+def _p2(n):
+    k = 1
+    while k < n:
+        k *= 2
+    return k
+
+
+def _alloc(topo, src, dsts):
+    allc = range(topo.CHIPS * topo.CORES_PER_CHIP)
+    far = [c for c in allc if topo.chip(c) != topo.chip(src)][0]
+    near = [c for c in allc if topo.chip(c) == topo.chip(src) and c != src][0]
+    low = _bits(topo.mask(src, far))
+    high = [b for b in _bits(topo.mask(src, near)) if b not in low]
+    off = [i for i, d in enumerate(dsts) if topo.chip(d) != topo.chip(src)]
+    on = [i for i, d in enumerate(dsts) if topo.chip(d) == topo.chip(src)]
+    out = [None] * len(dsts)
+    for idxs, pool in ((off, low), (on, high)):
+        if not idxs:
+            continue
+        per = len(pool) // _p2(len(idxs))
+        for j, i in enumerate(idxs):
+            out[i] = (sum(1 << b for b in pool[j * per:(j + 1) * per]), per)
+    return out
+
+
+def _plan(topo, cores):
+    n = len(cores)
+    allc = range(topo.CHIPS * topo.CORES_PER_CHIP)
+    helper, used = {}, set(cores)
+    for r, c in enumerate(cores):
+        far = [d for d in cores if d != c and not topo.may_write(c, d)]
+        if far:
+            cand = [h for h in allc if topo.chip(h) == topo.chip(c) and h not in used
+                    and all(topo.may_write(h, d) for d in far)]
+            cand.sort(key=lambda h: (topo.die(h) != topo.die(c), h))
+            helper[r] = cand[0]
+            used.add(cand[0])
+    groups, pos = [], []
+    for o, co in enumerate(cores):
+        near = [r for r in range(n) if r != o and topo.chip(cores[r]) == topo.chip(co)]
+        offc = [r for r in range(n) if topo.chip(cores[r]) != topo.chip(co)]
+        straight = [r for r in offc if topo.may_write(cores[r], co)]
+        straight.sort(key=lambda r: (not topo.may_write(co, cores[r]), r))
+        relayed = [r for r in offc if not topo.may_write(cores[r], co)]
+        gs = [[o] + near, straight, relayed]
+        groups.append(gs)
+        pos.append({r: i for i, r in enumerate(gs[0] + gs[1] + gs[2])})
+    cls = [{r: gi for gi in range(3) for r in groups[o][gi]} for o in range(n)]
+    req = []
+    for r, c in enumerate(cores):
+        st = [o for o in range(n) if o != r and topo.may_write(c, cores[o])]
+        via = [o for o in range(n) if o != r and not topo.may_write(c, cores[o])]
+        req.append({"st": st, "st_m": _alloc(topo, c, [cores[o] for o in st]), "via": via,
+                    "via_m": _alloc(topo, helper[r], [cores[o] for o in via]) if via else [],
+                    "h_m": _alloc(topo, c, [helper[r]])[0] if via else None})
+    rq_tot = [[0, 0, 0] for _ in range(n)]
+    for r in range(n):
+        for o, m in list(zip(req[r]["st"], req[r]["st_m"])) + list(zip(req[r]["via"], req[r]["via_m"])):
+            rq_tot[o][cls[o][r]] += m[1]
+    ans, rs_tot = [], [0] * n
+    for o, co in enumerate(cores):
+        calls, hslot = [], 0
+        for tg in (groups[o][0][1:] + groups[o][1], groups[o][2]):
+            dst = [cores[r] if topo.may_write(co, cores[r]) else helper[o] for r in tg]
+            ms = _alloc(topo, co, dst)
+            via = [r for r in tg if not topo.may_write(co, cores[r])]
+            vm = _alloc(topo, helper[o], [cores[r] for r in via]) if via else []
+            hs = {}
+            for r in via:
+                hs[r] = hslot
+                hslot += 1
+            calls.append({"tg": tg, "dst": dst, "m": ms, "via": via, "via_m": vm, "hs": hs})
+            for r, m in zip(tg, ms):
+                if r not in hs:
+                    rs_tot[r] += m[1]
+            for r, m in zip(via, vm):
+                rs_tot[r] += m[1]
+        ans.append(calls)
+    return {"helper": helper, "groups": groups, "pos": pos, "req": req, "rq_tot": rq_tot, "ans": ans,
+            "rs_tot": rs_tot}
+
+
+def _queue(eng, sem):
+    st = [0, 0]
+
+    def run(ins):
+        ins.then_inc(sem, 1)
+        st[0] += 1
+
+    def fence():
+        if st[1] < st[0]:
+            eng.wait_ge(sem, st[0])
+            st[1] = st[0]
+        return st[0]
+    return run, fence
+
+
+def _tr(topo, dst_core, mask, sem, src, dst):
+    rid, pid, _ = topo.addr(dst_core)
+    return RemoteDMATransfer(dst_ids=[DstId(rid=rid, pnc=pid)], dma_engine_mask=mask, remote_sem=sem, src=src, dst=dst)
+
+
+def _helper_program(g, T, topo, P, r):
+    s, cores, me = T.sem, list(T.cores), P["helper"][r]
+    rq = P["req"][r]
+    loc = 0
+    g.wait_ge(s.hqs, rq["h_m"][1])
+    trs = []
+    for o, m in zip(rq["via"], rq["via_m"]):
+        k = P["pos"][o][r]
+        gi = [i for i in range(3) if r in P["groups"][o][i]][0]
+        trs.append(_tr(topo, cores[o], m[0], s["rq%d" % gi], T.hq[:, 8 * o:8 * o + 8], T.reqL[:, 8 * k:8 * k + 8]))
+        loc += m[1]
+    g.remote_dma_fused(trs, local_sem=s.loc)
+    for ci, call in enumerate(P["ans"][r]):
+        if not call["via"]:
+            continue
+        g.wait_ge(s["hr%d" % (ci + 1)], sum(m[1] for t, m in zip(call["tg"], call["m"]) if t in call["hs"]))
+        trs = []
+        for t, m in zip(call["via"], call["via_m"]):
+            h = call["hs"][t]
+            trs.append(_tr(topo, cores[t], m[0], s.rs, T.hr[:, 64 * h:64 * h + 64], T.land[:, 64 * r:64 * r + 64]))
+            loc += m[1]
+        g.remote_dma_fused(trs, local_sem=s.loc)
+    g.wait_ge(s.loc, loc)
+
+
+def rank_program(g, core, T, topo):
+    cores = list(T.cores)
+    P = _plan(topo, cores)
+    me = T.rank_of(core)
+    if me is None:
+        for r, h in P["helper"].items():
+            if h == core:
+                _helper_program(g, T, topo, P, r)
+        return
+    A, s = AluOpType, T.sem
+    V, PE, AC, SY = g.vector, g.tensor, g.scalar, g.sync
+    v, vf = _queue(V, s.vq)
+    p, pf = _queue(PE, s.pq)
+    a, af = _queue(AC, s.aq)
+    q, qf = _queue(g, s.gq)
+    CP = ActivationFunctionType.Copy
+
+    SY.dma_start(T.ix[:], T.idx[:]).then_inc(s.dix, 16)
+    SY.dma_start(T.tabS[:], T.tab[:]).then_inc(s.dtab, 16)
+
+    v(V.memset(T.onesb[:], 1.0))
+    v(V.memset(T.ones64[:], 1.0))
+    v(V.memset(T.Hp[:, 0:24], 0.0))
+    v(V.memset(T.winT[:, 0:64], 0.0))
+    v(V.memset(T.winT[:, 2112:2176], 0.0))
+    v(V.memset(T.LT[:, 0:64], 0.0))
+    v(V.memset(T.LT[:, 576:640], 0.0))
+    q(g.iota(T.io8[:], [[1, 8]], 0, 0, allow_small_or_imprecise_dtypes=True))
+    q(g.iota(T.Di[:], [[1, 128]], 128, -1))
+    q(g.iota(T.pi[:], [[0, 1]], 0, 1))
+    m1 = qf()
+    g.wait_ge(s.vq, vf())
+    q(g.affine_select(T.Lb[:], T.onesb[:], [[1, 128]], A.is_ge, 0.0, -1, -1))
+    q(g.iota(T.ioOZ[:], [[1, 8], [0, 8]], 0, 0, allow_small_or_imprecise_dtypes=True))
+    q(g.iota(T.io128[:], [[1, 128]], 0, 0, allow_small_or_imprecise_dtypes=True))
+    q(g.affine_select(T.mz1[:], T.ones64[:], [[0, 8], [-16, 8]], A.is_ge, 0.0, 0, 1))
+    qf()
+    q(g.affine_select(T.mOZ[:], T.mz1[:], [[0, 8], [16, 8]], A.is_ge, 0.0, 15, -1))
+    m2 = qf()
+    V.wait_ge(s.gq, m1)
+    v(V.tensor_scalar(T.Da[:], T.Di[:], 15, None, op0=A.bitwise_and))
+    v(V.tensor_scalar(T.Ds[:], T.Di[:, 0:32], 31, None, op0=A.bitwise_and))
+    v(V.tensor_scalar(T.pa[:], T.pi[:], 5, None, op0=A.logical_shift_right))
+    vf()
+    v(V.tensor_scalar(T.Am[:], T.Da[:], 0.0, None, op0=A.is_equal))
+    v(V.tensor_scalar(T.S4[:], T.Ds[:], 0.0, None, op0=A.is_equal))
+    v(V.tensor_scalar(T.cmO[:], T.pa[:], 4096.0, -63.0, op0=A.mult, op1=A.add))
+    v(V.tensor_scalar(T.cmF[:], T.pa[:], 1024.0, -64.0, op0=A.mult, op1=A.add))
+
+    V.wait_ge(s.dix, 16)
+    v(V.tensor_scalar(T.oi[:], T.ix[:], 12, None, op0=A.logical_shift_right))
+    v(V.tensor_scalar(T.ti[:], T.ix[:], 31, None, op0=A.bitwise_and))
+    v(V.tensor_scalar(T.ki[:], T.ix[:], 5, 31, op0=A.logical_shift_right, op1=A.bitwise_and))
+    v(V.tensor_scalar(T.a1[:], T.ix[:], 3072, None, op0=A.bitwise_and))
+    vf()
+    v(V.tensor_copy(T.of[:], T.oi[:]))
+    vf()
+    for c in range(4):
+        v(V.tensor_scalar(T.Hp[:, 24 + 8 * c:32 + 8 * c], T.io8[:], T.of[:, c:c + 1], None, op0=A.is_equal))
+    PE.wait_ge(s.vq, vf())
+    PE.wait_ge(s.gq, m2)
+    p(PE.matmul(T.psS[:, 0:32], T.Lb[:], T.Hp[:, 24:56], True, False))
+    for d in (1, 2, 3):
+        p(PE.matmul(T.psS[:, 0:32], T.onesb[:], T.Hp[:, 24 - 8 * d:56 - 8 * d], False, d == 3))
+    v(V.tensor_scalar(T.v1[:], T.ti[:], 64.0, 1.0, op0=A.mult, op1=A.add))
+    v(V.tensor_scalar(T.v2[:], T.a1[:], 4.0, None, op0=A.mult))
+    v(V.tensor_copy(T.kf[:], T.ki[:]))
+    vf()
+    v(V.tensor_tensor(T.v3[:], T.v1[:], T.v2[:], A.add))
+    vf()
+    v(V.tensor_tensor(T.val[:], T.v3[:], T.kf[:], A.add))
+    vf()
+    V.wait_ge(s.gq, m2)
+    for c in range(4):
+        v(V.tensor_scalar(T.Rv[:, 64 * c:64 * c + 64], T.ioOZ[:], T.of[:, c:c + 1], T.val[:, c:c + 1],
+                          op0=A.is_equal, op1=A.mult))
+    V.wait_ge(s.pq, pf())
+    v(V.tensor_tensor(T.tmpS[:], T.Hp[:, 24:56], T.psS[:, 0:32], A.mult))
+    vf()
+    for c in range(4):
+        v(V.tensor_reduce(T.slot[:, c:c + 1], T.tmpS[:, 8 * c:8 * c + 8], AxisListType.X, A.add))
+    vf()
+    for c in range(4):
+        v(V.tensor_scalar(T.E[:, 128 * c:128 * c + 128], T.io128[:], T.slot[:, c:c + 1], None, op0=A.is_equal))
+    PE.wait_ge(s.vq, vf())
+    for c in range(4):
+        p(PE.matmul(T.psC[:, 0:64], T.E[:, 128 * c:128 * c + 128], T.Rv[:, 64 * c:64 * c + 64], c == 0, c == 3))
+    V.wait_ge(s.pq, pf())
+    v(V.tensor_tensor(T.reqS[:], T.psC[:, 0:64], T.mOZ[:], A.mult))
+    v(V.tensor_tensor(T.reqL[:, 0:8], T.psC[:, 8 * me:8 * me + 8], T.mOZ[:, 0:8], A.mult))
+    g.wait_ge(s.vq, vf())
+
+    loc = 0
+    rq = P["req"][me]
+    if rq["via"]:
+        rid, pid, _ = topo.addr(P["helper"][me])
+        g.remote_dma(T.hq[:], T.reqS[:], s.hqs, s.loc, pid, rid, rq["h_m"][0])
+        loc += rq["h_m"][1]
+    trs = []
+    for o, m in zip(rq["st"], rq["st_m"]):
+        k = P["pos"][o][me]
+        gi = [i for i in range(3) if me in P["groups"][o][i]][0]
+        trs.append(_tr(topo, cores[o], m[0], s["rq%d" % gi], T.reqS[:, 8 * o:8 * o + 8], T.reqL[:, 8 * k:8 * k + 8]))
+        loc += m[1]
+    g.remote_dma_fused(trs, local_sem=s.loc)
+
+    V.wait_ge(s.dtab, 16)
+    v(V.transpose(T.winT[:, 64:2112], T.tabS[:]))
+
+    k0 = 0
+    for gi, grp in enumerate(P["groups"][me]):
+        n = len(grp)
+        if n == 0:
+            continue
+        k1 = k0 + n
+        ps = T["psG%d" % gi]
+        if P["rq_tot"][me][gi]:
+            PE.wait_ge(s["rq%d" % gi], P["rq_tot"][me][gi])
+        PE.wait_ge(s.vq, vf())
+        p(PE.matmul(ps[:, 0:8 * n], T.Am[:], T.reqL[:, 8 * k0:8 * k1], True, True))
+        V.wait_ge(s.pq, pf())
+        v(V.tensor_scalar(T.t1[:, 8 * k0:8 * k1], ps[:, 0:8 * n], T.cmO[:, 0:1], 0.0, op0=A.subtract, op1=A.max))
+        vf()
+        v(V.tensor_scalar(T.off1[:, 8 * k0:8 * k1], T.t1[:, 8 * k0:8 * k1], 2112.0, None, op0=A.min))
+        AC.wait_ge(s.vq, vf())
+        for k in range(k0, k1):
+            ofs = T.off1[:, 8 * k:8 * k + 8]
+            v(V.tensor_copy(T.G[:, 128 * k:128 * k + 128], T.winT[:, 0:2144].indirect(ofs)))
+            a(AC.activation(T.G[:, 1024 + 128 * k:1024 + 128 * k + 128], T.winT[:, 32:2176].indirect(ofs), CP))
+            PE.wait_ge(s.vq, vf())
+            PE.wait_ge(s.aq, af())
+            for h in range(2):
+                c0 = 64 + 64 * (k - k0) + 32 * h
+                p(PE.matmul(ps[:, c0:c0 + 32], T.G[:, 1024 * h + 128 * k:1024 * h + 128 * k + 128], T.S4[:], True, True))
+        V.wait_ge(s.pq, pf())
+        if gi == 0:
+            v(V.tensor_copy(T.land[:, 64 * me:64 * me + 64], ps[:, 64:128]))
+            if n > 1:
+                v(V.tensor_copy(T.respS[:, 64:64 * n], ps[:, 128:64 + 64 * n]))
+        else:
+            v(V.tensor_copy(T.respS[:, 64 * k0:64 * k1], ps[:, 64:64 + 64 * n]))
+            call = P["ans"][me][gi - 1]
+            g.wait_ge(s.vq, vf())
+            trs = []
+            for t, d, m in zip(call["tg"], call["dst"], call["m"]):
+                k = P["pos"][me][t]
+                src = T.respS[:, 64 * k:64 * k + 64]
+                if t in call["hs"]:
+                    h = call["hs"][t]
+                    trs.append(_tr(topo, d, m[0], s["hr%d" % gi], src, T.hr[:, 64 * h:64 * h + 64]))
+                else:
+                    trs.append(_tr(topo, d, m[0], s.rs, src, T.land[:, 64 * me:64 * me + 64]))
+                loc += m[1]
+            g.remote_dma_fused(trs, local_sem=s.loc)
+        k0 = k1
+
+    v(V.tensor_copy(T.sli[:], T.slot[:]))
+    v(V.tensor_scalar(T.o64[:], T.of[:], 64.0, None, op0=A.mult))
+    vf()
+    v(V.tensor_scalar(T.hii[:], T.sli[:], 5, None, op0=A.logical_shift_right))
+    v(V.tensor_tensor(T.w2[:], T.o64[:], T.slot[:], A.add))
+    vf()
+    v(V.tensor_scalar(T.hif[:], T.hii[:], 992.0, None, op0=A.mult))
+    vf()
+    v(V.tensor_tensor(T.val2[:], T.w2[:], T.hif[:], A.add))
+    vf()
+    for c in range(4):
+        v(V.tensor_scalar(T.B2[:, 8 * c:8 * c + 8], T.mOZ[:, 0:8], T.val2[:, c:c + 1], None, op0=A.mult))
+    PE.wait_ge(s.vq, vf())
+    p(PE.matmul(T.psF[:, 0:32], T.Am[:], T.B2[:], True, True))
+    V.wait_ge(s.pq, pf())
+    v(V.tensor_scalar(T.t2[:], T.psF[:, 0:32], T.cmF[:, 0:1], 0.0, op0=A.subtract, op1=A.max))
+    vf()
+    v(V.tensor_scalar(T.off2[:], T.t2[:], 576.0, None, op0=A.min))
+    vf()
+
+    V.wait_ge(s.rs, P["rs_tot"][me])
+    v(V.transpose(T.LT[:, 64:576], T.land[:]))
+    AC.wait_ge(s.vq, vf())
+    v(V.tensor_copy(T.G2[:, 0:512], T.LT[:, 0:608].indirect(T.off2[:])))
+    a(AC.activation(T.G2[:, 512:1024], T.LT[:, 32:640].indirect(T.off2[:]), CP))
+    PE.wait_ge(s.vq, vf())
+    PE.wait_ge(s.aq, af())
+    for e in range(4):
+        for h in range(2):
+            p(PE.matmul(T.psY[:, 64 * e + 32 * h:64 * e + 32 * h + 32], T.G2[:, 512 * h + e:512 * h + 512:4], T.S4[:],
+                        True, True))
+    V.wait_ge(s.pq, pf())
+    v(V.tensor_copy(T.Ysb[:], T.psY[:, 0:256]))
+    SY.wait_ge(s.vq, vf())
+    SY.dma_start(T.y[:], T.Ysb[:]).then_inc(s.dy, 16)
+    g.wait_ge(s.loc, loc)
+    g.wait_ge(s.dy, 16)

@@ -2,6 +2,8 @@ import numpy as np
 from concourse.bass import DstId, RemoteDMATransfer
 from concourse.mybir import dt, AluOpType, AxisListType, ActivationFunctionType
 
+ALL_VIA = False
+
 F, I32, B16, U16 = "float32", "int32", "bfloat16", "uint16"
 SCRATCH = {
     "io8": ("sbuf", [128, 8], F), "ioOZ": ("sbuf", [128, 64], F), "io128": ("sbuf", [128, 128], F),
@@ -25,12 +27,14 @@ SCRATCH = {
     "w2": ("sbuf", [128, 4], F), "hif": ("sbuf", [128, 4], F), "val2": ("sbuf", [128, 4], F),
     "B2": ("sbuf", [128, 32], F), "t2": ("sbuf", [128, 32], F), "off2": ("sbuf", [128, 32], U16),
     "G2": ("sbuf", [128, 1024], F), "Ysb": ("sbuf", [128, 256], F),
-    "hq": ("sbuf", [128, 64], F), "hr": ("sbuf", [128, 256], F),
+    "hq": ("sbuf", [128, 64], F), "hr": ("sbuf", [128, 512], F),
     "psS": ("psum", [128, 512], F), "psC": ("psum", [128, 512], F), "psF": ("psum", [128, 512], F),
     "psY": ("psum", [128, 512], F), "psG0": ("psum", [128, 512], F), "psG1": ("psum", [128, 512], F),
     "psG2": ("psum", [128, 512], F),
 }
-SEMAPHORES = ["vq", "pq", "aq", "gq", "dix", "dtab", "dy", "rq0", "rq1", "rq2", "rs", "hqs", "hr1", "hr2", "loc"]
+SEMAPHORES = ["vq", "pq", "gq", "dix", "dtab", "dy", "rq0", "rq1", "rq2", "rs0", "rs1", "rs2", "hqs", "hr0",
+              "hr1", "hr2", "loc"] + ["gk%d" % i for i in range(8)] + [n + "%d" % i for n in ("mg", "rp") for i in range(3)] \
+    + [n + "%d" % i for n in ("fg", "fm", "ev") for i in range(4)]
 
 
 def _bits(mask):
@@ -44,22 +48,11 @@ def _p2(n):
     return k
 
 
-def _alloc(topo, src, dsts):
+def _alloc(topo, src, dsts, most=16):
     allc = range(topo.CHIPS * topo.CORES_PER_CHIP)
-    far = [c for c in allc if topo.chip(c) != topo.chip(src)][0]
-    near = [c for c in allc if topo.chip(c) == topo.chip(src) and c != src][0]
-    low = _bits(topo.mask(src, far))
-    high = [b for b in _bits(topo.mask(src, near)) if b not in low]
-    off = [i for i, d in enumerate(dsts) if topo.chip(d) != topo.chip(src)]
-    on = [i for i, d in enumerate(dsts) if topo.chip(d) == topo.chip(src)]
-    out = [None] * len(dsts)
-    for idxs, pool in ((off, low), (on, high)):
-        if not idxs:
-            continue
-        per = len(pool) // _p2(len(idxs))
-        for j, i in enumerate(idxs):
-            out[i] = (sum(1 << b for b in pool[j * per:(j + 1) * per]), per)
-    return out
+    pool = _bits(topo.mask(src, [c for c in allc if topo.chip(c) != topo.chip(src)][0]))
+    per = min(most, len(pool) // _p2(len(dsts)))
+    return [(sum(1 << b for b in pool[j * per:(j + 1) * per]), per) for j in range(len(dsts))]
 
 
 def _plan(topo, cores):
@@ -71,7 +64,7 @@ def _plan(topo, cores):
         if far:
             cand = [h for h in allc if topo.chip(h) == topo.chip(c) and h not in used
                     and all(topo.may_write(h, d) for d in far)]
-            cand.sort(key=lambda h: (topo.die(h) != topo.die(c), h))
+            cand.sort(key=lambda h: (topo.die(h) == topo.die(c), h))
             helper[r] = cand[0]
             used.add(cand[0])
     groups, pos = [], []
@@ -88,35 +81,43 @@ def _plan(topo, cores):
     req = []
     for r, c in enumerate(cores):
         st = [o for o in range(n) if o != r and topo.may_write(c, cores[o])]
+        onc = [o for o in st if topo.chip(cores[o]) == topo.chip(c)]
+        offc = sorted([o for o in st if topo.chip(cores[o]) != topo.chip(c)], key=lambda o: (o not in helper, o))
+        parts = [offc + onc]
         via = [o for o in range(n) if o != r and not topo.may_write(c, cores[o])]
-        req.append({"st": st, "st_m": _alloc(topo, c, [cores[o] for o in st]), "via": via,
+        req.append({"calls": [(pt, _alloc(topo, c, [cores[o] for o in pt])) for pt in parts], "via": via,
                     "via_m": _alloc(topo, helper[r], [cores[o] for o in via]) if via else [],
-                    "h_m": _alloc(topo, c, [helper[r]])[0] if via else None})
+                    "h_m": _alloc(topo, c, [helper[r]], 4)[0] if via else None})
     rq_tot = [[0, 0, 0] for _ in range(n)]
     for r in range(n):
-        for o, m in list(zip(req[r]["st"], req[r]["st_m"])) + list(zip(req[r]["via"], req[r]["via_m"])):
-            rq_tot[o][cls[o][r]] += m[1]
-    ans, rs_tot = [], [0] * n
+        for os_, ms in req[r]["calls"] + [(req[r]["via"], req[r]["via_m"])]:
+            for o, m in zip(os_, ms):
+                rq_tot[o][cls[o][r]] += m[1]
+    ans, rs_tot = [], [[0, 0, 0] for _ in range(n)]
+    late = [{} for _ in range(n)]
     for o, co in enumerate(cores):
         calls, hslot = [], 0
-        for tg in (groups[o][0][1:] + groups[o][1], groups[o][2]):
-            dst = [cores[r] if topo.may_write(co, cores[r]) else helper[o] for r in tg]
+        for tg in (groups[o][0][1:], groups[o][1], groups[o][2]):
+            via = [r for r in tg if not topo.may_write(co, cores[r])
+                   or (ALL_VIA and o in helper and topo.chip(cores[r]) != topo.chip(co))]
+            dst = [helper[o] if r in via else cores[r] for r in tg]
             ms = _alloc(topo, co, dst)
-            via = [r for r in tg if not topo.may_write(co, cores[r])]
             vm = _alloc(topo, helper[o], [cores[r] for r in via]) if via else []
             hs = {}
             for r in via:
                 hs[r] = hslot
                 hslot += 1
             calls.append({"tg": tg, "dst": dst, "m": ms, "via": via, "via_m": vm, "hs": hs})
+            for r in tg:
+                late[r][o] = (1 if r in groups[o][2] else 0) + (1 if r in hs else 0)
             for r, m in zip(tg, ms):
                 if r not in hs:
-                    rs_tot[r] += m[1]
+                    rs_tot[r][late[r][o]] += m[1]
             for r, m in zip(via, vm):
-                rs_tot[r] += m[1]
+                rs_tot[r][late[r][o]] += m[1]
         ans.append(calls)
-    return {"helper": helper, "groups": groups, "pos": pos, "req": req, "rq_tot": rq_tot, "ans": ans,
-            "rs_tot": rs_tot}
+    return {"helper": helper, "groups": groups, "pos": pos, "cls": cls, "req": req, "rq_tot": rq_tot, "ans": ans,
+            "rs_tot": rs_tot, "late": late}
 
 
 def _queue(eng, sem):
@@ -140,25 +141,23 @@ def _tr(topo, dst_core, mask, sem, src, dst):
 
 
 def _helper_program(g, T, topo, P, r):
-    s, cores, me = T.sem, list(T.cores), P["helper"][r]
-    rq = P["req"][r]
-    loc = 0
+    s, cores, rq, loc, trs = T.sem, list(T.cores), P["req"][r], 0, []
     g.wait_ge(s.hqs, rq["h_m"][1])
-    trs = []
     for o, m in zip(rq["via"], rq["via_m"]):
         k = P["pos"][o][r]
-        gi = [i for i in range(3) if r in P["groups"][o][i]][0]
-        trs.append(_tr(topo, cores[o], m[0], s["rq%d" % gi], T.hq[:, 8 * o:8 * o + 8], T.reqL[:, 8 * k:8 * k + 8]))
+        trs.append(_tr(topo, cores[o], m[0], s["rq%d" % P["cls"][o][r]], T.hq[:, 8 * o:8 * o + 8],
+                       T.reqL[:, 8 * k:8 * k + 8]))
         loc += m[1]
     g.remote_dma_fused(trs, local_sem=s.loc)
     for ci, call in enumerate(P["ans"][r]):
         if not call["via"]:
             continue
-        g.wait_ge(s["hr%d" % (ci + 1)], sum(m[1] for t, m in zip(call["tg"], call["m"]) if t in call["hs"]))
+        g.wait_ge(s["hr%d" % ci], sum(m[1] for t, m in zip(call["tg"], call["m"]) if t in call["hs"]))
         trs = []
         for t, m in zip(call["via"], call["via_m"]):
             h = call["hs"][t]
-            trs.append(_tr(topo, cores[t], m[0], s.rs, T.hr[:, 64 * h:64 * h + 64], T.land[:, 64 * r:64 * r + 64]))
+            trs.append(_tr(topo, cores[t], m[0], s["rs%d" % P["late"][t][r]], T.hr[:, 64 * h:64 * h + 64],
+                           T.land[:, 64 * r:64 * r + 64]))
             loc += m[1]
         g.remote_dma_fused(trs, local_sem=s.loc)
     g.wait_ge(s.loc, loc)
@@ -177,7 +176,6 @@ def rank_program(g, core, T, topo):
     V, PE, AC, SY = g.vector, g.tensor, g.scalar, g.sync
     v, vf = _queue(V, s.vq)
     p, pf = _queue(PE, s.pq)
-    a, af = _queue(AC, s.aq)
     q, qf = _queue(g, s.gq)
     CP = ActivationFunctionType.Copy
 
@@ -220,7 +218,11 @@ def rank_program(g, core, T, topo):
     v(V.tensor_scalar(T.a1[:], T.ix[:], 3072, None, op0=A.bitwise_and))
     vf()
     v(V.tensor_copy(T.of[:], T.oi[:]))
+    v(V.tensor_scalar(T.v1[:], T.ti[:], 64.0, 1.0, op0=A.mult, op1=A.add))
+    v(V.tensor_scalar(T.v2[:], T.a1[:], 4.0, None, op0=A.mult))
+    v(V.tensor_copy(T.kf[:], T.ki[:]))
     vf()
+    v(V.tensor_tensor(T.v3[:], T.v1[:], T.v2[:], A.add))
     for c in range(4):
         v(V.tensor_scalar(T.Hp[:, 24 + 8 * c:32 + 8 * c], T.io8[:], T.of[:, c:c + 1], None, op0=A.is_equal))
     PE.wait_ge(s.vq, vf())
@@ -228,12 +230,6 @@ def rank_program(g, core, T, topo):
     p(PE.matmul(T.psS[:, 0:32], T.Lb[:], T.Hp[:, 24:56], True, False))
     for d in (1, 2, 3):
         p(PE.matmul(T.psS[:, 0:32], T.onesb[:], T.Hp[:, 24 - 8 * d:56 - 8 * d], False, d == 3))
-    v(V.tensor_scalar(T.v1[:], T.ti[:], 64.0, 1.0, op0=A.mult, op1=A.add))
-    v(V.tensor_scalar(T.v2[:], T.a1[:], 4.0, None, op0=A.mult))
-    v(V.tensor_copy(T.kf[:], T.ki[:]))
-    vf()
-    v(V.tensor_tensor(T.v3[:], T.v1[:], T.v2[:], A.add))
-    vf()
     v(V.tensor_tensor(T.val[:], T.v3[:], T.kf[:], A.add))
     vf()
     V.wait_ge(s.gq, m2)
@@ -262,20 +258,33 @@ def rank_program(g, core, T, topo):
         rid, pid, _ = topo.addr(P["helper"][me])
         g.remote_dma(T.hq[:], T.reqS[:], s.hqs, s.loc, pid, rid, rq["h_m"][0])
         loc += rq["h_m"][1]
-    trs = []
-    for o, m in zip(rq["st"], rq["st_m"]):
-        k = P["pos"][o][me]
-        gi = [i for i in range(3) if me in P["groups"][o][i]][0]
-        trs.append(_tr(topo, cores[o], m[0], s["rq%d" % gi], T.reqS[:, 8 * o:8 * o + 8], T.reqL[:, 8 * k:8 * k + 8]))
-        loc += m[1]
-    g.remote_dma_fused(trs, local_sem=s.loc)
+    for os_, ms in rq["calls"]:
+        trs = []
+        for o, m in zip(os_, ms):
+            k = P["pos"][o][me]
+            trs.append(_tr(topo, cores[o], m[0], s["rq%d" % P["cls"][o][me]], T.reqS[:, 8 * o:8 * o + 8],
+                           T.reqL[:, 8 * k:8 * k + 8]))
+            loc += m[1]
+        g.remote_dma_fused(trs, local_sem=s.loc)
 
     V.wait_ge(s.dtab, 16)
     v(V.transpose(T.winT[:, 64:2112], T.tabS[:]))
 
-    k0 = 0
-    for gi, grp in enumerate(P["groups"][me]):
-        n = len(grp)
+    def _b2():
+        for c in range(4):
+            v(V.tensor_scalar(T.B2[:, 8 * c:8 * c + 8], T.mOZ[:, 0:8], T.val2[:, c:c + 1], None, op0=A.mult))
+    prep = [
+        lambda: (v(V.tensor_copy(T.sli[:], T.slot[:])), v(V.tensor_scalar(T.o64[:], T.of[:], 64.0, None, op0=A.mult))),
+        lambda: (v(V.tensor_scalar(T.hii[:], T.sli[:], 5, None, op0=A.logical_shift_right)),
+                 v(V.tensor_tensor(T.w2[:], T.o64[:], T.slot[:], A.add))),
+        lambda: v(V.tensor_scalar(T.hif[:], T.hii[:], 992.0, None, op0=A.mult)),
+        lambda: v(V.tensor_tensor(T.val2[:], T.w2[:], T.hif[:], A.add)),
+        _b2,
+    ]
+
+    sizes = [len(x) for x in P["groups"][me]]
+    for gi in (0, 1, 2):
+        n, k0 = sizes[gi], sum(sizes[:gi])
         if n == 0:
             continue
         k1 = k0 + n
@@ -283,29 +292,33 @@ def rank_program(g, core, T, topo):
         if P["rq_tot"][me][gi]:
             PE.wait_ge(s["rq%d" % gi], P["rq_tot"][me][gi])
         PE.wait_ge(s.vq, vf())
-        p(PE.matmul(ps[:, 0:8 * n], T.Am[:], T.reqL[:, 8 * k0:8 * k1], True, True))
-        V.wait_ge(s.pq, pf())
+        PE.matmul(ps[:, 0:8 * n], T.Am[:], T.reqL[:, 8 * k0:8 * k1], True, True).then_inc(s["rp%d" % gi], 1)
+        V.wait_ge(s["rp%d" % gi], 1)
         v(V.tensor_scalar(T.t1[:, 8 * k0:8 * k1], ps[:, 0:8 * n], T.cmO[:, 0:1], 0.0, op0=A.subtract, op1=A.max))
         vf()
         v(V.tensor_scalar(T.off1[:, 8 * k0:8 * k1], T.t1[:, 8 * k0:8 * k1], 2112.0, None, op0=A.min))
         AC.wait_ge(s.vq, vf())
         for k in range(k0, k1):
-            ofs = T.off1[:, 8 * k:8 * k + 8]
-            v(V.tensor_copy(T.G[:, 128 * k:128 * k + 128], T.winT[:, 0:2144].indirect(ofs)))
-            a(AC.activation(T.G[:, 1024 + 128 * k:1024 + 128 * k + 128], T.winT[:, 32:2176].indirect(ofs), CP))
-            PE.wait_ge(s.vq, vf())
-            PE.wait_ge(s.aq, af())
+            ofs, gk = T.off1[:, 8 * k:8 * k + 8], s["gk%d" % k]
+            V.tensor_copy(T.G[:, 128 * k:128 * k + 128], T.winT[:, 0:2144].indirect(ofs)).then_inc(gk, 1)
+            AC.activation(T.G[:, 1024 + 128 * k:1024 + 128 * k + 128], T.winT[:, 32:2176].indirect(ofs), CP).then_inc(gk, 1)
+            PE.wait_ge(gk, 2)
             for h in range(2):
                 c0 = 64 + 64 * (k - k0) + 32 * h
-                p(PE.matmul(ps[:, c0:c0 + 32], T.G[:, 1024 * h + 128 * k:1024 * h + 128 * k + 128], T.S4[:], True, True))
-        V.wait_ge(s.pq, pf())
+                PE.matmul(ps[:, c0:c0 + 32], T.G[:, 1024 * h + 128 * k:1024 * h + 128 * k + 128], T.S4[:], True,
+                          True).then_inc(s["mg%d" % gi], 1)
+            if prep:
+                vf()
+                prep.pop(0)()
+        V.wait_ge(s["mg%d" % gi], 2 * n)
         if gi == 0:
-            v(V.tensor_copy(T.land[:, 64 * me:64 * me + 64], ps[:, 64:128]))
             if n > 1:
                 v(V.tensor_copy(T.respS[:, 64:64 * n], ps[:, 128:64 + 64 * n]))
+            v(V.tensor_copy(T.land[:, 64 * me:64 * me + 64], ps[:, 64:128]))
         else:
             v(V.tensor_copy(T.respS[:, 64 * k0:64 * k1], ps[:, 64:64 + 64 * n]))
-            call = P["ans"][me][gi - 1]
+        call = P["ans"][me][gi]
+        if call["tg"]:
             g.wait_ge(s.vq, vf())
             trs = []
             for t, d, m in zip(call["tg"], call["dst"], call["m"]):
@@ -315,23 +328,13 @@ def rank_program(g, core, T, topo):
                     h = call["hs"][t]
                     trs.append(_tr(topo, d, m[0], s["hr%d" % gi], src, T.hr[:, 64 * h:64 * h + 64]))
                 else:
-                    trs.append(_tr(topo, d, m[0], s.rs, src, T.land[:, 64 * me:64 * me + 64]))
+                    trs.append(_tr(topo, d, m[0], s["rs%d" % P["late"][t][me]], src, T.land[:, 64 * me:64 * me + 64]))
                 loc += m[1]
             g.remote_dma_fused(trs, local_sem=s.loc)
-        k0 = k1
 
-    v(V.tensor_copy(T.sli[:], T.slot[:]))
-    v(V.tensor_scalar(T.o64[:], T.of[:], 64.0, None, op0=A.mult))
-    vf()
-    v(V.tensor_scalar(T.hii[:], T.sli[:], 5, None, op0=A.logical_shift_right))
-    v(V.tensor_tensor(T.w2[:], T.o64[:], T.slot[:], A.add))
-    vf()
-    v(V.tensor_scalar(T.hif[:], T.hii[:], 992.0, None, op0=A.mult))
-    vf()
-    v(V.tensor_tensor(T.val2[:], T.w2[:], T.hif[:], A.add))
-    vf()
-    for c in range(4):
-        v(V.tensor_scalar(T.B2[:, 8 * c:8 * c + 8], T.mOZ[:, 0:8], T.val2[:, c:c + 1], None, op0=A.mult))
+    while prep:
+        vf()
+        prep.pop(0)()
     PE.wait_ge(s.vq, vf())
     p(PE.matmul(T.psF[:, 0:32], T.Am[:], T.B2[:], True, True))
     V.wait_ge(s.pq, pf())
@@ -340,20 +343,28 @@ def rank_program(g, core, T, topo):
     v(V.tensor_scalar(T.off2[:], T.t2[:], 576.0, None, op0=A.min))
     vf()
 
-    V.wait_ge(s.rs, P["rs_tot"][me])
-    v(V.transpose(T.LT[:, 64:576], T.land[:]))
+    v(V.transpose(T.LT[:, 64 + 64 * me:128 + 64 * me], T.land[:, 64 * me:64 * me + 64]))
+    for lt in range(3):
+        if P["rs_tot"][me][lt]:
+            V.wait_ge(s["rs%d" % lt], P["rs_tot"][me][lt])
+        for o in range(len(cores)):
+            if o != me and P["late"][me][o] == lt:
+                v(V.transpose(T.LT[:, 64 + 64 * o:128 + 64 * o], T.land[:, 64 * o:64 * o + 64]))
     AC.wait_ge(s.vq, vf())
-    v(V.tensor_copy(T.G2[:, 0:512], T.LT[:, 0:608].indirect(T.off2[:])))
-    a(AC.activation(T.G2[:, 512:1024], T.LT[:, 32:640].indirect(T.off2[:]), CP))
-    PE.wait_ge(s.vq, vf())
-    PE.wait_ge(s.aq, af())
-    for e in range(4):
+    banks = [T.psY, T.psS, T.psC, T.psF]
+    for c in range(4):
+        ofs, fg = T.off2[:, 8 * c:8 * c + 8], s["fg%d" % c]
+        V.tensor_copy(T.G2[:, 128 * c:128 * c + 128], T.LT[:, 0:608].indirect(ofs)).then_inc(fg, 1)
+        AC.activation(T.G2[:, 512 + 128 * c:512 + 128 * c + 128], T.LT[:, 32:640].indirect(ofs), CP).then_inc(fg, 1)
+        PE.wait_ge(fg, 2)
         for h in range(2):
-            p(PE.matmul(T.psY[:, 64 * e + 32 * h:64 * e + 32 * h + 32], T.G2[:, 512 * h + e:512 * h + 512:4], T.S4[:],
-                        True, True))
-    V.wait_ge(s.pq, pf())
-    v(V.tensor_copy(T.Ysb[:], T.psY[:, 0:256]))
-    SY.wait_ge(s.vq, vf())
-    SY.dma_start(T.y[:], T.Ysb[:]).then_inc(s.dy, 16)
+            PE.matmul(banks[c][:, 32 * h:32 * h + 32], T.G2[:, 512 * h + 128 * c:512 * h + 128 * c + 128], T.S4[:],
+                      True, True).then_inc(s["fm%d" % c], 1)
+    for c in range(4):
+        V.wait_ge(s["fm%d" % c], 2)
+        V.tensor_copy(T.Ysb[:, 64 * c:64 * c + 64], banks[c][:, 0:64]).then_inc(s["ev%d" % c], 1)
+        Q = SY if c % 2 == 0 else AC
+        Q.wait_ge(s["ev%d" % c], 1)
+        Q.dma_start(T.y[128 * c:128 * c + 128, :], T.Ysb[:, 64 * c:64 * c + 64]).then_inc(s.dy, 16)
     g.wait_ge(s.loc, loc)
-    g.wait_ge(s.dy, 16)
+    g.wait_ge(s.dy, 64)

@@ -6,7 +6,7 @@ ALL_VIA = False
 
 F, I32, B16, U16 = "float32", "int32", "bfloat16", "uint16"
 SCRATCH = {
-    "io8": ("sbuf", [128, 8], F), "ioOZ": ("sbuf", [128, 64], F), "io128": ("sbuf", [128, 128], F),
+    "io8": ("sbuf", [128, 8], F), "ioOZ": ("sbuf", [128, 64], F), "io128": ("sbuf", [128, 128], B16),
     "onesb": ("sbuf", [128, 128], B16), "Lb": ("sbuf", [128, 128], B16),
     "ones64": ("sbuf", [128, 64], F), "mz1": ("sbuf", [128, 64], F), "mOZ": ("sbuf", [128, 64], F),
     "Di": ("sbuf", [128, 128], I32), "Da": ("sbuf", [128, 128], I32), "Am": ("sbuf", [128, 128], F),
@@ -16,16 +16,17 @@ SCRATCH = {
     "ix": ("sbuf", [128, 4], I32), "oi": ("sbuf", [128, 4], I32), "ti": ("sbuf", [128, 4], I32),
     "ki": ("sbuf", [128, 4], I32), "a1": ("sbuf", [128, 4], I32),
     "of": ("sbuf", [128, 4], F), "v1": ("sbuf", [128, 4], F), "v2": ("sbuf", [128, 4], F),
-    "kf": ("sbuf", [128, 4], F), "v3": ("sbuf", [128, 4], F), "val": ("sbuf", [128, 4], F),
-    "Hp": ("sbuf", [128, 56], B16), "Rv": ("sbuf", [128, 256], F), "tmpS": ("sbuf", [128, 32], F),
-    "slot": ("sbuf", [128, 4], F), "E": ("sbuf", [128, 512], F), "reqS": ("sbuf", [128, 64], F),
+    "kf": ("sbuf", [128, 4], F), "v3": ("sbuf", [128, 4], F),
+    "Hp": ("sbuf", [128, 56], B16), "Rv": ("sbuf", [128, 512], B16), "tmpS": ("sbuf", [128, 32], F),
+    "Rm": ("sbuf", [128, 32], F), "scn": ("sbuf", [128, 32], F), "E": ("sbuf", [128, 512], B16),
+    "reqS": ("sbuf", [128, 64], F),
     "tabS": ("sbuf", [128, 2048], F), "winT": ("sbuf", [128, 2176], F), "reqL": ("sbuf", [128, 64], F),
-    "t1": ("sbuf", [128, 64], F), "off1": ("sbuf", [128, 64], U16), "G": ("sbuf", [128, 2048], F),
+    "off1": ("sbuf", [128, 64], U16), "G": ("sbuf", [128, 2048], F),
     "respS": ("sbuf", [128, 512], F),
     "land": ("sbuf", [128, 512], F), "LT": ("sbuf", [128, 640], F),
     "sli": ("sbuf", [128, 4], I32), "hii": ("sbuf", [128, 4], I32), "o64": ("sbuf", [128, 4], F),
     "w2": ("sbuf", [128, 4], F), "hif": ("sbuf", [128, 4], F), "val2": ("sbuf", [128, 4], F),
-    "B2": ("sbuf", [128, 32], F), "t2": ("sbuf", [128, 32], F), "off2": ("sbuf", [128, 32], U16),
+    "B2": ("sbuf", [128, 32], F), "off2": ("sbuf", [128, 32], U16),
     "G2": ("sbuf", [128, 1024], F), "Ysb": ("sbuf", [128, 256], F),
     "hq": ("sbuf", [128, 64], F), "hr": ("sbuf", [128, 512], F),
     "psS": ("psum", [128, 512], F), "psC": ("psum", [128, 512], F), "psF": ("psum", [128, 512], F),
@@ -189,19 +190,24 @@ def rank_program(g, core, T, topo):
     v(V.memset(T.winT[:, 2112:2176], 0.0))
     v(V.memset(T.LT[:, 0:64], 0.0))
     v(V.memset(T.LT[:, 576:640], 0.0))
+    v(V.memset(T.Rm[:], 1.0))
     q(g.iota(T.io8[:], [[1, 8]], 0, 0, allow_small_or_imprecise_dtypes=True))
     q(g.iota(T.Di[:], [[1, 128]], 128, -1))
     q(g.iota(T.pi[:], [[0, 1]], 0, 1))
     m1 = qf()
     g.wait_ge(s.vq, vf())
     q(g.affine_select(T.Lb[:], T.onesb[:], [[1, 128]], A.is_ge, 0.0, -1, -1))
+    mL = qf()
     q(g.iota(T.ioOZ[:], [[1, 8], [0, 8]], 0, 0, allow_small_or_imprecise_dtypes=True))
+    mO = qf()
     q(g.iota(T.io128[:], [[1, 128]], 0, 0, allow_small_or_imprecise_dtypes=True))
     q(g.affine_select(T.mz1[:], T.ones64[:], [[0, 8], [-16, 8]], A.is_ge, 0.0, 0, 1))
     qf()
     q(g.affine_select(T.mOZ[:], T.mz1[:], [[0, 8], [16, 8]], A.is_ge, 0.0, 15, -1))
     m2 = qf()
     V.wait_ge(s.gq, m1)
+    for c in range(4):
+        v(V.memset(T.Rm[:, 8 * c:8 * c + 1], 0.0))
     v(V.tensor_scalar(T.Da[:], T.Di[:], 15, None, op0=A.bitwise_and))
     v(V.tensor_scalar(T.Ds[:], T.Di[:, 0:32], 31, None, op0=A.bitwise_and))
     v(V.tensor_scalar(T.pa[:], T.pi[:], 5, None, op0=A.logical_shift_right))
@@ -218,39 +224,40 @@ def rank_program(g, core, T, topo):
     v(V.tensor_scalar(T.a1[:], T.ix[:], 3072, None, op0=A.bitwise_and))
     vf()
     v(V.tensor_copy(T.of[:], T.oi[:]))
-    v(V.tensor_scalar(T.v1[:], T.ti[:], 64.0, 1.0, op0=A.mult, op1=A.add))
+    v(V.tensor_scalar(T.v1[:], T.ti[:], 64.0, None, op0=A.mult))
     v(V.tensor_scalar(T.v2[:], T.a1[:], 4.0, None, op0=A.mult))
-    v(V.tensor_copy(T.kf[:], T.ki[:]))
+    v(V.tensor_scalar(T.kf[:], T.ki[:], 1.0, None, op0=A.add))
     vf()
     v(V.tensor_tensor(T.v3[:], T.v1[:], T.v2[:], A.add))
     for c in range(4):
         v(V.tensor_scalar(T.Hp[:, 24 + 8 * c:32 + 8 * c], T.io8[:], T.of[:, c:c + 1], None, op0=A.is_equal))
     PE.wait_ge(s.vq, vf())
-    PE.wait_ge(s.gq, m2)
+    PE.wait_ge(s.gq, mL)
     p(PE.matmul(T.psS[:, 0:32], T.Lb[:], T.Hp[:, 24:56], True, False))
     for d in (1, 2, 3):
         p(PE.matmul(T.psS[:, 0:32], T.onesb[:], T.Hp[:, 24 - 8 * d:56 - 8 * d], False, d == 3))
-    v(V.tensor_tensor(T.val[:], T.v3[:], T.kf[:], A.add))
-    vf()
-    V.wait_ge(s.gq, m2)
+    V.wait_ge(s.gq, mO)
     for c in range(4):
-        v(V.tensor_scalar(T.Rv[:, 64 * c:64 * c + 64], T.ioOZ[:], T.of[:, c:c + 1], T.val[:, c:c + 1],
-                          op0=A.is_equal, op1=A.mult))
+        for h, part in enumerate((T.v3, T.kf)):
+            v(V.tensor_scalar(T.Rv[:, 128 * c + 64 * h:128 * c + 64 * h + 64], T.ioOZ[:], T.of[:, c:c + 1],
+                              part[:, c:c + 1], op0=A.is_equal, op1=A.mult))
     V.wait_ge(s.pq, pf())
     v(V.tensor_tensor(T.tmpS[:], T.Hp[:, 24:56], T.psS[:, 0:32], A.mult))
     vf()
-    for c in range(4):
-        v(V.tensor_reduce(T.slot[:, c:c + 1], T.tmpS[:, 8 * c:8 * c + 8], AxisListType.X, A.add))
+    v(V.tensor_tensor_scan(T.scn[:], T.Rm[:], T.tmpS[:], 0.0, A.mult, A.add))
     vf()
+    V.wait_ge(s.gq, m2)
     for c in range(4):
-        v(V.tensor_scalar(T.E[:, 128 * c:128 * c + 128], T.io128[:], T.slot[:, c:c + 1], None, op0=A.is_equal))
+        v(V.tensor_scalar(T.E[:, 128 * c:128 * c + 128], T.io128[:], T.scn[:, 8 * c + 7:8 * c + 8], None, op0=A.is_equal))
     PE.wait_ge(s.vq, vf())
     for c in range(4):
-        p(PE.matmul(T.psC[:, 0:64], T.E[:, 128 * c:128 * c + 128], T.Rv[:, 64 * c:64 * c + 64], c == 0, c == 3))
+        for h in range(2):
+            p(PE.matmul(T.psC[:, 0:64], T.E[:, 128 * c:128 * c + 128], T.Rv[:, 128 * c + 64 * h:128 * c + 64 * h + 64],
+                        c == 0 and h == 0, c == 3 and h == 1))
     V.wait_ge(s.pq, pf())
     v(V.tensor_tensor(T.reqS[:], T.psC[:, 0:64], T.mOZ[:], A.mult))
-    v(V.tensor_tensor(T.reqL[:, 0:8], T.psC[:, 8 * me:8 * me + 8], T.mOZ[:, 0:8], A.mult))
     g.wait_ge(s.vq, vf())
+    v(V.tensor_tensor(T.reqL[:, 0:8], T.psC[:, 8 * me:8 * me + 8], T.mOZ[:, 0:8], A.mult))
 
     loc = 0
     rq = P["req"][me]
@@ -274,9 +281,9 @@ def rank_program(g, core, T, topo):
         for c in range(4):
             v(V.tensor_scalar(T.B2[:, 8 * c:8 * c + 8], T.mOZ[:, 0:8], T.val2[:, c:c + 1], None, op0=A.mult))
     prep = [
-        lambda: (v(V.tensor_copy(T.sli[:], T.slot[:])), v(V.tensor_scalar(T.o64[:], T.of[:], 64.0, None, op0=A.mult))),
+        lambda: (v(V.tensor_copy(T.sli[:], T.scn[:, 7:32:8])), v(V.tensor_scalar(T.o64[:], T.of[:], 64.0, None, op0=A.mult))),
         lambda: (v(V.tensor_scalar(T.hii[:], T.sli[:], 5, None, op0=A.logical_shift_right)),
-                 v(V.tensor_tensor(T.w2[:], T.o64[:], T.slot[:], A.add))),
+                 v(V.tensor_tensor(T.w2[:], T.o64[:], T.scn[:, 7:32:8], A.add))),
         lambda: v(V.tensor_scalar(T.hif[:], T.hii[:], 992.0, None, op0=A.mult)),
         lambda: v(V.tensor_tensor(T.val2[:], T.w2[:], T.hif[:], A.add)),
         _b2,
@@ -294,9 +301,7 @@ def rank_program(g, core, T, topo):
         PE.wait_ge(s.vq, vf())
         PE.matmul(ps[:, 0:8 * n], T.Am[:], T.reqL[:, 8 * k0:8 * k1], True, True).then_inc(s["rp%d" % gi], 1)
         V.wait_ge(s["rp%d" % gi], 1)
-        v(V.tensor_scalar(T.t1[:, 8 * k0:8 * k1], ps[:, 0:8 * n], T.cmO[:, 0:1], 0.0, op0=A.subtract, op1=A.max))
-        vf()
-        v(V.tensor_scalar(T.off1[:, 8 * k0:8 * k1], T.t1[:, 8 * k0:8 * k1], 2112.0, None, op0=A.min))
+        v(V.tensor_scalar(T.off1[:, 8 * k0:8 * k1], ps[:, 0:8 * n], T.cmO[:, 0:1], 2112.0, op0=A.subtract, op1=A.min))
         AC.wait_ge(s.vq, vf())
         for k in range(k0, k1):
             ofs, gk = T.off1[:, 8 * k:8 * k + 8], s["gk%d" % k]
@@ -338,9 +343,7 @@ def rank_program(g, core, T, topo):
     PE.wait_ge(s.vq, vf())
     p(PE.matmul(T.psF[:, 0:32], T.Am[:], T.B2[:], True, True))
     V.wait_ge(s.pq, pf())
-    v(V.tensor_scalar(T.t2[:], T.psF[:, 0:32], T.cmF[:, 0:1], 0.0, op0=A.subtract, op1=A.max))
-    vf()
-    v(V.tensor_scalar(T.off2[:], T.t2[:], 576.0, None, op0=A.min))
+    v(V.tensor_scalar(T.off2[:], T.psF[:, 0:32], T.cmF[:, 0:1], 576.0, op0=A.subtract, op1=A.min))
     vf()
 
     v(V.transpose(T.LT[:, 64 + 64 * me:128 + 64 * me], T.land[:, 64 * me:64 * me + 64]))

@@ -2,8 +2,6 @@ import numpy as np
 from concourse.bass import DstId, RemoteDMATransfer
 from concourse.mybir import dt, AluOpType, AxisListType, ActivationFunctionType
 
-ALL_VIA = False
-
 F, I32, B16, U16 = "float32", "int32", "bfloat16", "uint16"
 SCRATCH = {
     "io8": ("sbuf", [128, 8], F), "ioOZ": ("sbuf", [128, 64], F), "io128": ("sbuf", [128, 128], B16),
@@ -28,14 +26,16 @@ SCRATCH = {
     "w2": ("sbuf", [128, 4], F), "hif": ("sbuf", [128, 4], F), "val2": ("sbuf", [128, 4], F),
     "B2": ("sbuf", [128, 32], F), "off2": ("sbuf", [128, 32], U16),
     "G2": ("sbuf", [128, 1024], F), "Ysb": ("sbuf", [128, 256], F),
-    "hq": ("sbuf", [128, 64], F), "hr": ("sbuf", [128, 512], F),
+    "hq": ("sbuf", [128, 64], F),
     "psS": ("psum", [128, 512], F), "psC": ("psum", [128, 512], F), "psF": ("psum", [128, 512], F),
     "psY": ("psum", [128, 512], F), "psG0": ("psum", [128, 512], F), "psG1": ("psum", [128, 512], F),
     "psG2": ("psum", [128, 512], F),
 }
-SEMAPHORES = ["vq", "pq", "gq", "dix", "dtab", "dy", "rq0", "rq1", "rq2", "rs0", "rs1", "rs2", "hqs", "hr0",
-              "hr1", "hr2", "loc"] + ["gk%d" % i for i in range(8)] + [n + "%d" % i for n in ("mg", "rp") for i in range(3)] \
-    + [n + "%d" % i for n in ("fg", "fm", "ev") for i in range(4)]
+SEMAPHORES = ["vq", "pq", "gq", "dix", "dy", "rq0", "rq1", "rq2", "rs0", "rs1", "hqs", "loc"] \
+    + ["gk%d" % i for i in range(8)] + [n + "%d" % i for n in ("mg", "rp") for i in range(3)] \
+    + [n + "%d" % i for n in ("fg", "fm", "ev", "dt", "st") for i in range(4)]
+NQ = 4
+EARLY = 3
 
 
 def _bits(mask):
@@ -49,9 +49,20 @@ def _p2(n):
     return k
 
 
-def _alloc(topo, src, dsts, most=16):
+def _low2(bits):
+    k = 1
+    while 2 * k <= len(bits):
+        k *= 2
+    return (sum(1 << b for b in bits[:k]), k)
+
+
+def _offmask(topo, src):
     allc = range(topo.CHIPS * topo.CORES_PER_CHIP)
-    pool = _bits(topo.mask(src, [c for c in allc if topo.chip(c) != topo.chip(src)][0]))
+    return topo.mask(src, [c for c in allc if topo.chip(c) != topo.chip(src)][0])
+
+
+def _alloc(topo, src, dsts, most=16):
+    pool = _bits(_offmask(topo, src))
     per = min(most, len(pool) // _p2(len(dsts)))
     return [(sum(1 << b for b in pool[j * per:(j + 1) * per]), per) for j in range(len(dsts))]
 
@@ -59,66 +70,54 @@ def _alloc(topo, src, dsts, most=16):
 def _plan(topo, cores):
     n = len(cores)
     allc = range(topo.CHIPS * topo.CORES_PER_CHIP)
-    helper, used = {}, set(cores)
+    helper, used, stage = {}, set(cores), {}
     for r, c in enumerate(cores):
         far = [d for d in cores if d != c and not topo.may_write(c, d)]
         if far:
             cand = [h for h in allc if topo.chip(h) == topo.chip(c) and h not in used
                     and all(topo.may_write(h, d) for d in far)]
-            cand.sort(key=lambda h: (topo.die(h) == topo.die(c), h))
+            cand.sort(key=lambda h: (topo.die(h) != topo.die(c), h))
             helper[r] = cand[0]
             used.add(cand[0])
-    groups, pos = [], []
+            on = topo.mask(c, cand[0])
+            only = _bits(on & ~_offmask(topo, c)) or _bits(on)
+            stage[r] = [_low2(_bits(on)) if qd < NQ // 2 else _low2(only) for qd in range(NQ)]
+    srv = [[helper[o] if (o in helper and r != o and not topo.may_write(cores[o], cores[r])) else cores[o]
+            for r in range(n)] for o in range(n)]
+    sv = {}
     for o, co in enumerate(cores):
-        near = [r for r in range(n) if r != o and topo.chip(cores[r]) == topo.chip(co)]
-        offc = [r for r in range(n) if topo.chip(cores[r]) != topo.chip(co)]
-        straight = [r for r in offc if topo.may_write(cores[r], co)]
-        straight.sort(key=lambda r: (not topo.may_write(co, cores[r]), r))
-        relayed = [r for r in offc if not topo.may_write(cores[r], co)]
-        gs = [[o] + near, straight, relayed]
-        groups.append(gs)
-        pos.append({r: i for i, r in enumerate(gs[0] + gs[1] + gs[2])})
-    cls = [{r: gi for gi in range(3) for r in groups[o][gi]} for o in range(n)]
+        for sc in sorted(set(srv[o])):
+            mine = [r for r in range(n) if srv[o][r] == sc]
+            g0 = ([o] if sc == co else []) + [r for r in mine if r != o and topo.chip(cores[r]) == topo.chip(sc)]
+            offc = [r for r in mine if topo.chip(cores[r]) != topo.chip(sc)]
+            g1 = [r for r in offc if topo.may_write(cores[r], sc)]
+            g2 = [r for r in offc if not topo.may_write(cores[r], sc)]
+            sv[sc] = {"o": o, "groups": [g0, g1, g2], "pos": {r: i for i, r in enumerate(g0 + g1 + g2)},
+                      "cls": {r: gi for gi, gg in enumerate((g0, g1, g2)) for r in gg}, "rq_tot": [0, 0, 0]}
     req = []
     for r, c in enumerate(cores):
-        st = [o for o in range(n) if o != r and topo.may_write(c, cores[o])]
-        onc = [o for o in st if topo.chip(cores[o]) == topo.chip(c)]
-        offc = sorted([o for o in st if topo.chip(cores[o]) != topo.chip(c)], key=lambda o: (o not in helper, o))
-        parts = [offc + onc]
-        via = [o for o in range(n) if o != r and not topo.may_write(c, cores[o])]
-        req.append({"calls": [(pt, _alloc(topo, c, [cores[o] for o in pt])) for pt in parts], "via": via,
-                    "via_m": _alloc(topo, helper[r], [cores[o] for o in via]) if via else [],
+        st = [o for o in range(n) if o != r and topo.may_write(c, srv[o][r])]
+        st.sort(key=lambda o: (topo.chip(srv[o][r]) == topo.chip(c), o))
+        via = [o for o in range(n) if o != r and not topo.may_write(c, srv[o][r])]
+        st_m = _alloc(topo, c, [srv[o][r] for o in st])
+        via_m = _alloc(topo, helper[r], [srv[o][r] for o in via]) if via else []
+        req.append({"st": st, "st_m": st_m, "via": via, "via_m": via_m,
                     "h_m": _alloc(topo, c, [helper[r]], 4)[0] if via else None})
-    rq_tot = [[0, 0, 0] for _ in range(n)]
-    for r in range(n):
-        for os_, ms in req[r]["calls"] + [(req[r]["via"], req[r]["via_m"])]:
-            for o, m in zip(os_, ms):
-                rq_tot[o][cls[o][r]] += m[1]
-    ans, rs_tot = [], [[0, 0, 0] for _ in range(n)]
+        for o, m in zip(st + via, st_m + via_m):
+            S = sv[srv[o][r]]
+            S["rq_tot"][S["cls"][r]] += m[1]
+    rs_tot = [[0, 0] for _ in range(n)]
     late = [{} for _ in range(n)]
-    for o, co in enumerate(cores):
-        calls, hslot = [], 0
-        for tg in (groups[o][0][1:], groups[o][1], groups[o][2]):
-            via = [r for r in tg if not topo.may_write(co, cores[r])
-                   or (ALL_VIA and o in helper and topo.chip(cores[r]) != topo.chip(co))]
-            dst = [helper[o] if r in via else cores[r] for r in tg]
-            ms = _alloc(topo, co, dst)
-            vm = _alloc(topo, helper[o], [cores[r] for r in via]) if via else []
-            hs = {}
-            for r in via:
-                hs[r] = hslot
-                hslot += 1
-            calls.append({"tg": tg, "dst": dst, "m": ms, "via": via, "via_m": vm, "hs": hs})
-            for r in tg:
-                late[r][o] = (1 if r in groups[o][2] else 0) + (1 if r in hs else 0)
+    for sc, S in sv.items():
+        S["ans"] = []
+        for gi, gg in enumerate(S["groups"]):
+            tg = [r for r in gg if r != S["o"]]
+            ms = _alloc(topo, sc, [cores[r] for r in tg]) if tg else []
+            S["ans"].append({"tg": tg, "m": ms})
             for r, m in zip(tg, ms):
-                if r not in hs:
-                    rs_tot[r][late[r][o]] += m[1]
-            for r, m in zip(via, vm):
-                rs_tot[r][late[r][o]] += m[1]
-        ans.append(calls)
-    return {"helper": helper, "groups": groups, "pos": pos, "cls": cls, "req": req, "rq_tot": rq_tot, "ans": ans,
-            "rs_tot": rs_tot, "late": late}
+                late[r][S["o"]] = 1 if gi == 2 else 0
+                rs_tot[r][late[r][S["o"]]] += m[1]
+    return {"helper": helper, "stage": stage, "srv": srv, "sv": sv, "req": req, "rs_tot": rs_tot, "late": late}
 
 
 def _queue(eng, sem):
@@ -141,27 +140,94 @@ def _tr(topo, dst_core, mask, sem, src, dst):
     return RemoteDMATransfer(dst_ids=[DstId(rid=rid, pnc=pid)], dma_engine_mask=mask, remote_sem=sem, src=src, dst=dst)
 
 
-def _helper_program(g, T, topo, P, r):
-    s, cores, rq, loc, trs = T.sem, list(T.cores), P["req"][r], 0, []
+def _serve(g, T, topo, P, core, v, vf, prep, loc):
+    A, s, cores = AluOpType, T.sem, list(T.cores)
+    V, PE, AC = g.vector, g.tensor, g.scalar
+    CP = ActivationFunctionType.Copy
+    S = P["sv"][core]
+    o = S["o"]
+    own = cores[o] == core
+    sizes = [len(x) for x in S["groups"]]
+    for gi in (0, 1, 2):
+        n, k0 = sizes[gi], sum(sizes[:gi])
+        if n == 0:
+            continue
+        k1 = k0 + n
+        ps = T["psG%d" % gi]
+        if S["rq_tot"][gi]:
+            PE.wait_ge(s["rq%d" % gi], S["rq_tot"][gi])
+        PE.wait_ge(s.vq, vf())
+        PE.matmul(ps[:, 0:8 * n], T.Am[:], T.reqL[:, 8 * k0:8 * k1], True, True).then_inc(s["rp%d" % gi], 1)
+        V.wait_ge(s["rp%d" % gi], 1)
+        v(V.tensor_scalar(T.off1[:, 8 * k0:8 * k1], ps[:, 0:8 * n], T.cmO[:, 0:1], 2112.0, op0=A.subtract, op1=A.min))
+        AC.wait_ge(s.vq, vf())
+        for k in range(k0, k1):
+            ofs, gk = T.off1[:, 8 * k:8 * k + 8], s["gk%d" % k]
+            V.tensor_copy(T.G[:, 128 * k:128 * k + 128], T.winT[:, 0:2144].indirect(ofs)).then_inc(gk, 1)
+            AC.activation(T.G[:, 1024 + 128 * k:1024 + 128 * k + 128], T.winT[:, 32:2176].indirect(ofs), CP).then_inc(gk, 1)
+            PE.wait_ge(gk, 2)
+            for h in range(2):
+                c0 = 64 + 64 * (k - k0) + 32 * h
+                PE.matmul(ps[:, c0:c0 + 32], T.G[:, 1024 * h + 128 * k:1024 * h + 128 * k + 128], T.S4[:], True,
+                          True).then_inc(s["mg%d" % gi], 1)
+            if prep:
+                vf()
+                prep.pop(0)()
+        V.wait_ge(s["mg%d" % gi], 2 * n)
+        if gi == 0 and own:
+            if n > 1:
+                v(V.tensor_copy(T.respS[:, 64:64 * n], ps[:, 128:64 + 64 * n]))
+            v(V.tensor_copy(T.land[:, 64 * o:64 * o + 64], ps[:, 64:128]))
+        else:
+            v(V.tensor_copy(T.respS[:, 64 * k0:64 * k1], ps[:, 64:64 + 64 * n]))
+        call = S["ans"][gi]
+        if call["tg"]:
+            g.wait_ge(s.vq, vf())
+            trs = []
+            for t, m in zip(call["tg"], call["m"]):
+                k = S["pos"][t]
+                trs.append(_tr(topo, cores[t], m[0], s["rs%d" % P["late"][t][o]], T.respS[:, 64 * k:64 * k + 64],
+                               T.land[:, 64 * o:64 * o + 64]))
+                loc[0] += m[1]
+            g.remote_dma_fused(trs, local_sem=s.loc)
+
+
+def _server_consts(g, T, v, vf, q, qf):
+    A, V = AluOpType, g.vector
+    v(V.tensor_scalar(T.Da[:], T.Di[:], 15, None, op0=A.bitwise_and))
+    v(V.tensor_scalar(T.Ds[:], T.Di[:, 0:32], 31, None, op0=A.bitwise_and))
+    v(V.tensor_scalar(T.pa[:], T.pi[:], 5, None, op0=A.logical_shift_right))
+    vf()
+    v(V.tensor_scalar(T.Am[:], T.Da[:], 0.0, None, op0=A.is_equal))
+    v(V.tensor_scalar(T.S4[:], T.Ds[:], 0.0, None, op0=A.is_equal))
+    v(V.tensor_scalar(T.cmO[:], T.pa[:], 2048.0, -63.0, op0=A.mult, op1=A.add))
+
+
+def _helper_program(g, T, topo, P, r, core):
+    s, cores, rq, loc, trs = T.sem, list(T.cores), P["req"][r], [0], []
+    V = g.vector
+    v, vf = _queue(V, s.vq)
+    q, qf = _queue(g, s.gq)
+    v(V.memset(T.winT[:, 0:64], 0.0))
+    v(V.memset(T.winT[:, 2112:2176], 0.0))
+    q(g.iota(T.Di[:], [[1, 128]], 128, -1))
+    q(g.iota(T.pi[:], [[0, 1]], 0, 1))
+    V.wait_ge(s.gq, qf())
+    _server_consts(g, T, v, vf, q, qf)
     g.wait_ge(s.hqs, rq["h_m"][1])
     for o, m in zip(rq["via"], rq["via_m"]):
-        k = P["pos"][o][r]
-        trs.append(_tr(topo, cores[o], m[0], s["rq%d" % P["cls"][o][r]], T.hq[:, 8 * o:8 * o + 8],
+        S = P["sv"][P["srv"][o][r]]
+        k = S["pos"][r]
+        trs.append(_tr(topo, P["srv"][o][r], m[0], s["rq%d" % S["cls"][r]], T.hq[:, 8 * o:8 * o + 8],
                        T.reqL[:, 8 * k:8 * k + 8]))
-        loc += m[1]
+        loc[0] += m[1]
     g.remote_dma_fused(trs, local_sem=s.loc)
-    for ci, call in enumerate(P["ans"][r]):
-        if not call["via"]:
-            continue
-        g.wait_ge(s["hr%d" % ci], sum(m[1] for t, m in zip(call["tg"], call["m"]) if t in call["hs"]))
-        trs = []
-        for t, m in zip(call["via"], call["via_m"]):
-            h = call["hs"][t]
-            trs.append(_tr(topo, cores[t], m[0], s["rs%d" % P["late"][t][r]], T.hr[:, 64 * h:64 * h + 64],
-                           T.land[:, 64 * r:64 * r + 64]))
-            loc += m[1]
-        g.remote_dma_fused(trs, local_sem=s.loc)
-    g.wait_ge(s.loc, loc)
+    w = 2048 // NQ
+    for qd in range(NQ):
+        V.wait_ge(s["st%d" % qd], P["stage"][r][qd][1])
+        v(V.transpose(T.winT[:, 64 + w * qd:64 + w * qd + w], T.tabS[:, w * qd:w * qd + w]))
+    _serve(g, T, topo, P, core, v, vf, [], loc)
+    g.wait_ge(s.loc, loc[0])
 
 
 def rank_program(g, core, T, topo):
@@ -171,7 +237,7 @@ def rank_program(g, core, T, topo):
     if me is None:
         for r, h in P["helper"].items():
             if h == core:
-                _helper_program(g, T, topo, P, r)
+                _helper_program(g, T, topo, P, r, core)
         return
     A, s = AluOpType, T.sem
     V, PE, AC, SY = g.vector, g.tensor, g.scalar, g.sync
@@ -179,9 +245,23 @@ def rank_program(g, core, T, topo):
     p, pf = _queue(PE, s.pq)
     q, qf = _queue(g, s.gq)
     CP = ActivationFunctionType.Copy
+    loc = [0]
+    w = 2048 // NQ
+    rp = w // 64
 
     SY.dma_start(T.ix[:], T.idx[:]).then_inc(s.dix, 16)
-    SY.dma_start(T.tabS[:], T.tab[:]).then_inc(s.dtab, 16)
+    for qd in range(NQ):
+        for a in range(4):
+            r0 = 1024 * a + 32 * rp * qd
+            (SY if a < 2 else AC).dma_start(T.tabS[32 * a:32 * a + 32, w * qd:w * qd + w],
+                                            T.tab[r0:r0 + 32 * rp, :]).then_inc(s["dt%d" % qd], 16)
+
+    def stage(qd):
+        m = P["stage"][me][qd]
+        rid, pid, _ = topo.addr(P["helper"][me])
+        g.wait_ge(s["dt%d" % qd], 64)
+        g.remote_dma(T.tabS[:, w * qd:w * qd + w], T.tabS[:, w * qd:w * qd + w], s["st%d" % qd], s.loc, pid, rid, m[0])
+        loc[0] += m[1]
 
     v(V.memset(T.onesb[:], 1.0))
     v(V.memset(T.ones64[:], 1.0))
@@ -205,27 +285,24 @@ def rank_program(g, core, T, topo):
     qf()
     q(g.affine_select(T.mOZ[:], T.mz1[:], [[0, 8], [16, 8]], A.is_ge, 0.0, 15, -1))
     m2 = qf()
+    if me in P["helper"]:
+        for qd in range(EARLY):
+            stage(qd)
     V.wait_ge(s.gq, m1)
     for c in range(4):
         v(V.memset(T.Rm[:, 8 * c:8 * c + 1], 0.0))
-    v(V.tensor_scalar(T.Da[:], T.Di[:], 15, None, op0=A.bitwise_and))
-    v(V.tensor_scalar(T.Ds[:], T.Di[:, 0:32], 31, None, op0=A.bitwise_and))
-    v(V.tensor_scalar(T.pa[:], T.pi[:], 5, None, op0=A.logical_shift_right))
-    vf()
-    v(V.tensor_scalar(T.Am[:], T.Da[:], 0.0, None, op0=A.is_equal))
-    v(V.tensor_scalar(T.S4[:], T.Ds[:], 0.0, None, op0=A.is_equal))
-    v(V.tensor_scalar(T.cmO[:], T.pa[:], 4096.0, -63.0, op0=A.mult, op1=A.add))
+    _server_consts(g, T, v, vf, q, qf)
     v(V.tensor_scalar(T.cmF[:], T.pa[:], 1024.0, -64.0, op0=A.mult, op1=A.add))
 
     V.wait_ge(s.dix, 16)
     v(V.tensor_scalar(T.oi[:], T.ix[:], 12, None, op0=A.logical_shift_right))
-    v(V.tensor_scalar(T.ti[:], T.ix[:], 31, None, op0=A.bitwise_and))
-    v(V.tensor_scalar(T.ki[:], T.ix[:], 5, 31, op0=A.logical_shift_right, op1=A.bitwise_and))
-    v(V.tensor_scalar(T.a1[:], T.ix[:], 3072, None, op0=A.bitwise_and))
+    v(V.tensor_scalar(T.ti[:], T.ix[:], 7, None, op0=A.bitwise_and))
+    v(V.tensor_scalar(T.ki[:], T.ix[:], 3, 31, op0=A.logical_shift_right, op1=A.bitwise_and))
+    v(V.tensor_scalar(T.a1[:], T.ix[:], 3840, None, op0=A.bitwise_and))
     vf()
     v(V.tensor_copy(T.of[:], T.oi[:]))
     v(V.tensor_scalar(T.v1[:], T.ti[:], 64.0, None, op0=A.mult))
-    v(V.tensor_scalar(T.v2[:], T.a1[:], 4.0, None, op0=A.mult))
+    v(V.tensor_scalar(T.v2[:], T.a1[:], 2.0, None, op0=A.mult))
     v(V.tensor_scalar(T.kf[:], T.ki[:], 1.0, None, op0=A.add))
     vf()
     v(V.tensor_tensor(T.v3[:], T.v1[:], T.v2[:], A.add))
@@ -259,22 +336,25 @@ def rank_program(g, core, T, topo):
     g.wait_ge(s.vq, vf())
     v(V.tensor_tensor(T.reqL[:, 0:8], T.psC[:, 8 * me:8 * me + 8], T.mOZ[:, 0:8], A.mult))
 
-    loc = 0
     rq = P["req"][me]
     if rq["via"]:
         rid, pid, _ = topo.addr(P["helper"][me])
         g.remote_dma(T.hq[:], T.reqS[:], s.hqs, s.loc, pid, rid, rq["h_m"][0])
-        loc += rq["h_m"][1]
-    for os_, ms in rq["calls"]:
-        trs = []
-        for o, m in zip(os_, ms):
-            k = P["pos"][o][me]
-            trs.append(_tr(topo, cores[o], m[0], s["rq%d" % P["cls"][o][me]], T.reqS[:, 8 * o:8 * o + 8],
-                           T.reqL[:, 8 * k:8 * k + 8]))
-            loc += m[1]
-        g.remote_dma_fused(trs, local_sem=s.loc)
+        loc[0] += rq["h_m"][1]
+    trs = []
+    for o, m in zip(rq["st"], rq["st_m"]):
+        S = P["sv"][P["srv"][o][me]]
+        k = S["pos"][me]
+        trs.append(_tr(topo, P["srv"][o][me], m[0], s["rq%d" % S["cls"][me]], T.reqS[:, 8 * o:8 * o + 8],
+                       T.reqL[:, 8 * k:8 * k + 8]))
+        loc[0] += m[1]
+    g.remote_dma_fused(trs, local_sem=s.loc)
+    if me in P["helper"]:
+        for qd in range(EARLY, NQ):
+            stage(qd)
 
-    V.wait_ge(s.dtab, 16)
+    for qd in range(NQ):
+        V.wait_ge(s["dt%d" % qd], 64)
     v(V.transpose(T.winT[:, 64:2112], T.tabS[:]))
 
     def _b2():
@@ -289,53 +369,7 @@ def rank_program(g, core, T, topo):
         _b2,
     ]
 
-    sizes = [len(x) for x in P["groups"][me]]
-    for gi in (0, 1, 2):
-        n, k0 = sizes[gi], sum(sizes[:gi])
-        if n == 0:
-            continue
-        k1 = k0 + n
-        ps = T["psG%d" % gi]
-        if P["rq_tot"][me][gi]:
-            PE.wait_ge(s["rq%d" % gi], P["rq_tot"][me][gi])
-        PE.wait_ge(s.vq, vf())
-        PE.matmul(ps[:, 0:8 * n], T.Am[:], T.reqL[:, 8 * k0:8 * k1], True, True).then_inc(s["rp%d" % gi], 1)
-        V.wait_ge(s["rp%d" % gi], 1)
-        v(V.tensor_scalar(T.off1[:, 8 * k0:8 * k1], ps[:, 0:8 * n], T.cmO[:, 0:1], 2112.0, op0=A.subtract, op1=A.min))
-        AC.wait_ge(s.vq, vf())
-        for k in range(k0, k1):
-            ofs, gk = T.off1[:, 8 * k:8 * k + 8], s["gk%d" % k]
-            V.tensor_copy(T.G[:, 128 * k:128 * k + 128], T.winT[:, 0:2144].indirect(ofs)).then_inc(gk, 1)
-            AC.activation(T.G[:, 1024 + 128 * k:1024 + 128 * k + 128], T.winT[:, 32:2176].indirect(ofs), CP).then_inc(gk, 1)
-            PE.wait_ge(gk, 2)
-            for h in range(2):
-                c0 = 64 + 64 * (k - k0) + 32 * h
-                PE.matmul(ps[:, c0:c0 + 32], T.G[:, 1024 * h + 128 * k:1024 * h + 128 * k + 128], T.S4[:], True,
-                          True).then_inc(s["mg%d" % gi], 1)
-            if prep:
-                vf()
-                prep.pop(0)()
-        V.wait_ge(s["mg%d" % gi], 2 * n)
-        if gi == 0:
-            if n > 1:
-                v(V.tensor_copy(T.respS[:, 64:64 * n], ps[:, 128:64 + 64 * n]))
-            v(V.tensor_copy(T.land[:, 64 * me:64 * me + 64], ps[:, 64:128]))
-        else:
-            v(V.tensor_copy(T.respS[:, 64 * k0:64 * k1], ps[:, 64:64 + 64 * n]))
-        call = P["ans"][me][gi]
-        if call["tg"]:
-            g.wait_ge(s.vq, vf())
-            trs = []
-            for t, d, m in zip(call["tg"], call["dst"], call["m"]):
-                k = P["pos"][me][t]
-                src = T.respS[:, 64 * k:64 * k + 64]
-                if t in call["hs"]:
-                    h = call["hs"][t]
-                    trs.append(_tr(topo, d, m[0], s["hr%d" % gi], src, T.hr[:, 64 * h:64 * h + 64]))
-                else:
-                    trs.append(_tr(topo, d, m[0], s["rs%d" % P["late"][t][me]], src, T.land[:, 64 * me:64 * me + 64]))
-                loc += m[1]
-            g.remote_dma_fused(trs, local_sem=s.loc)
+    _serve(g, T, topo, P, core, v, vf, prep, loc)
 
     while prep:
         vf()
@@ -347,7 +381,7 @@ def rank_program(g, core, T, topo):
     vf()
 
     v(V.transpose(T.LT[:, 64 + 64 * me:128 + 64 * me], T.land[:, 64 * me:64 * me + 64]))
-    for lt in range(3):
+    for lt in range(2):
         if P["rs_tot"][me][lt]:
             V.wait_ge(s["rs%d" % lt], P["rs_tot"][me][lt])
         for o in range(len(cores)):
@@ -369,5 +403,5 @@ def rank_program(g, core, T, topo):
         Q = SY if c % 2 == 0 else AC
         Q.wait_ge(s["ev%d" % c], 1)
         Q.dma_start(T.y[128 * c:128 * c + 128, :], T.Ysb[:, 64 * c:64 * c + 64]).then_inc(s.dy, 16)
-    g.wait_ge(s.loc, loc)
+    g.wait_ge(s.loc, loc[0])
     g.wait_ge(s.dy, 64)

import numpy as np
from concourse.bass import DstId, RemoteDMATransfer
from concourse.mybir import dt, AluOpType, AxisListType, ActivationFunctionType

F, I32, B16, U16 = "float32", "int32", "bfloat16", "uint16"
SCRATCH = {
    "io8": ("sbuf", [128, 8], F), "ioOZ": ("sbuf", [128, 64], F), "io128": ("sbuf", [128, 128], B16),
    "onesb": ("sbuf", [128, 128], B16), "Lb": ("sbuf", [128, 128], B16),
    "ones64": ("sbuf", [128, 64], F), "mz1": ("sbuf", [128, 64], F), "mOZ": ("sbuf", [128, 64], F),
    "Di": ("sbuf", [128, 128], I32), "Da": ("sbuf", [128, 128], I32), "Am": ("sbuf", [128, 128], F),
    "Ds": ("sbuf", [128, 32], I32), "S4": ("sbuf", [128, 32], F),
    "pi": ("sbuf", [128, 1], I32), "pa": ("sbuf", [128, 1], I32),
    "cmO": ("sbuf", [128, 1], F), "cmF": ("sbuf", [128, 1], F),
    "ix": ("sbuf", [128, 4], I32), "oi": ("sbuf", [128, 4], I32), "ti": ("sbuf", [128, 4], I32),
    "ki": ("sbuf", [128, 4], I32), "a1": ("sbuf", [128, 4], I32),
    "of": ("sbuf", [128, 4], F), "v1": ("sbuf", [128, 4], F), "v2": ("sbuf", [128, 4], F),
    "kf": ("sbuf", [128, 4], F), "v3": ("sbuf", [128, 4], F),
    "Hp": ("sbuf", [128, 56], B16), "Rv": ("sbuf", [128, 512], B16), "tmpS": ("sbuf", [128, 32], F),
    "Rm": ("sbuf", [128, 32], F), "scn": ("sbuf", [128, 32], F), "E": ("sbuf", [128, 512], B16),
    "reqS": ("sbuf", [128, 64], F),
    "tabS": ("sbuf", [128, 2048], F), "winT": ("sbuf", [128, 2176], F), "reqL": ("sbuf", [128, 64], F),
    "off1": ("sbuf", [128, 64], U16), "G": ("sbuf", [128, 2048], F),
    "respS": ("sbuf", [128, 512], F),
    "land": ("sbuf", [128, 512], F), "LT": ("sbuf", [128, 640], F),
    "sli": ("sbuf", [128, 4], I32), "hii": ("sbuf", [128, 4], I32), "o64": ("sbuf", [128, 4], F),
    "w2": ("sbuf", [128, 4], F), "hif": ("sbuf", [128, 4], F), "val2": ("sbuf", [128, 4], F),
    "B2": ("sbuf", [128, 32], F), "off2": ("sbuf", [128, 32], U16),
    "G2": ("sbuf", [128, 1024], F), "Ysb": ("sbuf", [128, 256], F),
    "hq": ("sbuf", [128, 64], F),
    "psS": ("psum", [128, 512], F), "psC": ("psum", [128, 512], F), "psF": ("psum", [128, 512], F),
    "psY": ("psum", [128, 512], F), "psG0": ("psum", [128, 512], F), "psG1": ("psum", [128, 512], F),
    "psG2": ("psum", [128, 512], F),
}
SEMAPHORES = ["vq", "pq", "gq", "dix", "dy", "rq0", "rq1", "rq2", "rs0", "rs1", "hqs", "loc"] \
    + ["gk%d" % i for i in range(8)] + [n + "%d" % i for n in ("mg", "rp") for i in range(3)] \
    + [n + "%d" % i for n in ("fg", "fm", "ev", "dt", "st") for i in range(4)]
NQ = 4
EARLY = 3


def _bits(mask):
    return [b for b in range(16) if (mask >> b) & 1]


def _p2(n):
    k = 1
    while k < n:
        k *= 2
    return k


def _low2(bits):
    k = 1
    while 2 * k <= len(bits):
        k *= 2
    return (sum(1 << b for b in bits[:k]), k)


def _offmask(topo, src):
    allc = range(topo.CHIPS * topo.CORES_PER_CHIP)
    return topo.mask(src, [c for c in allc if topo.chip(c) != topo.chip(src)][0])


def _alloc(topo, src, dsts, most=16):
    pool = _bits(_offmask(topo, src))
    per = min(most, len(pool) // _p2(len(dsts)))
    return [(sum(1 << b for b in pool[j * per:(j + 1) * per]), per) for j in range(len(dsts))]


def _plan(topo, cores):
    n = len(cores)
    allc = range(topo.CHIPS * topo.CORES_PER_CHIP)
    helper, used, stage = {}, set(cores), {}
    for r, c in enumerate(cores):
        far = [d for d in cores if d != c and not topo.may_write(c, d)]
        if far:
            cand = [h for h in allc if topo.chip(h) == topo.chip(c) and h not in used
                    and all(topo.may_write(h, d) for d in far)]
            cand.sort(key=lambda h: (topo.die(h) != topo.die(c), h))
            helper[r] = cand[0]
            used.add(cand[0])
            on = topo.mask(c, cand[0])
            only = _bits(on & ~_offmask(topo, c)) or _bits(on)
            stage[r] = [_low2(_bits(on)) if qd < NQ // 2 else _low2(only) for qd in range(NQ)]
    srv = [[helper[o] if (o in helper and r != o and not topo.may_write(cores[o], cores[r])) else cores[o]
            for r in range(n)] for o in range(n)]
    sv = {}
    for o, co in enumerate(cores):
        for sc in sorted(set(srv[o])):
            mine = [r for r in range(n) if srv[o][r] == sc]
            g0 = ([o] if sc == co else []) + [r for r in mine if r != o and topo.chip(cores[r]) == topo.chip(sc)]
            offc = [r for r in mine if topo.chip(cores[r]) != topo.chip(sc)]
            g1 = [r for r in offc if topo.may_write(cores[r], sc)]
            g2 = [r for r in offc if not topo.may_write(cores[r], sc)]
            sv[sc] = {"o": o, "groups": [g0, g1, g2], "pos": {r: i for i, r in enumerate(g0 + g1 + g2)},
                      "cls": {r: gi for gi, gg in enumerate((g0, g1, g2)) for r in gg}, "rq_tot": [0, 0, 0]}
    req = []
    for r, c in enumerate(cores):
        st = [o for o in range(n) if o != r and topo.may_write(c, srv[o][r])]
        st.sort(key=lambda o: (topo.chip(srv[o][r]) == topo.chip(c), o))
        via = [o for o in range(n) if o != r and not topo.may_write(c, srv[o][r])]
        st_m = _alloc(topo, c, [srv[o][r] for o in st])
        via_m = _alloc(topo, helper[r], [srv[o][r] for o in via]) if via else []
        req.append({"st": st, "st_m": st_m, "via": via, "via_m": via_m,
                    "h_m": _alloc(topo, c, [helper[r]], 4)[0] if via else None})
        for o, m in zip(st + via, st_m + via_m):
            S = sv[srv[o][r]]
            S["rq_tot"][S["cls"][r]] += m[1]
    rs_tot = [[0, 0] for _ in range(n)]
    late = [{} for _ in range(n)]
    for sc, S in sv.items():
        S["ans"] = []
        for gi, gg in enumerate(S["groups"]):
            tg = [r for r in gg if r != S["o"]]
            ms = _alloc(topo, sc, [cores[r] for r in tg]) if tg else []
            S["ans"].append({"tg": tg, "m": ms})
            for r, m in zip(tg, ms):
                late[r][S["o"]] = 1 if gi == 2 else 0
                rs_tot[r][late[r][S["o"]]] += m[1]
    return {"helper": helper, "stage": stage, "srv": srv, "sv": sv, "req": req, "rs_tot": rs_tot, "late": late}


def _queue(eng, sem):
    st = [0, 0]

    def run(ins):
        ins.then_inc(sem, 1)
        st[0] += 1

    def fence():
        if st[1] < st[0]:
            eng.wait_ge(sem, st[0])
            st[1] = st[0]
        return st[0]
    return run, fence


def _tr(topo, dst_core, mask, sem, src, dst):
    rid, pid, _ = topo.addr(dst_core)
    return RemoteDMATransfer(dst_ids=[DstId(rid=rid, pnc=pid)], dma_engine_mask=mask, remote_sem=sem, src=src, dst=dst)


def _serve(g, T, topo, P, core, v, vf, prep, loc):
    A, s, cores = AluOpType, T.sem, list(T.cores)
    V, PE, AC = g.vector, g.tensor, g.scalar
    CP = ActivationFunctionType.Copy
    S = P["sv"][core]
    o = S["o"]
    own = cores[o] == core
    sizes = [len(x) for x in S["groups"]]
    for gi in (0, 1, 2):
        n, k0 = sizes[gi], sum(sizes[:gi])
        if n == 0:
            continue
        k1 = k0 + n
        ps = T["psG%d" % gi]
        if S["rq_tot"][gi]:
            PE.wait_ge(s["rq%d" % gi], S["rq_tot"][gi])
        PE.wait_ge(s.vq, vf())
        PE.matmul(ps[:, 0:8 * n], T.Am[:], T.reqL[:, 8 * k0:8 * k1], True, True).then_inc(s["rp%d" % gi], 1)
        V.wait_ge(s["rp%d" % gi], 1)
        v(V.tensor_scalar(T.off1[:, 8 * k0:8 * k1], ps[:, 0:8 * n], T.cmO[:, 0:1], 2112.0, op0=A.subtract, op1=A.min))
        AC.wait_ge(s.vq, vf())
        for k in range(k0, k1):
            ofs, gk = T.off1[:, 8 * k:8 * k + 8], s["gk%d" % k]
            V.tensor_copy(T.G[:, 128 * k:128 * k + 128], T.winT[:, 0:2144].indirect(ofs)).then_inc(gk, 1)
            AC.activation(T.G[:, 1024 + 128 * k:1024 + 128 * k + 128], T.winT[:, 32:2176].indirect(ofs), CP).then_inc(gk, 1)
            PE.wait_ge(gk, 2)
            for h in range(2):
                c0 = 64 + 64 * (k - k0) + 32 * h
                PE.matmul(ps[:, c0:c0 + 32], T.G[:, 1024 * h + 128 * k:1024 * h + 128 * k + 128], T.S4[:], True,
                          True).then_inc(s["mg%d" % gi], 1)
            if prep:
                vf()
                prep.pop(0)()
        V.wait_ge(s["mg%d" % gi], 2 * n)
        if gi == 0 and own:
            if n > 1:
                v(V.tensor_copy(T.respS[:, 64:64 * n], ps[:, 128:64 + 64 * n]))
            v(V.tensor_copy(T.land[:, 64 * o:64 * o + 64], ps[:, 64:128]))
        else:
            v(V.tensor_copy(T.respS[:, 64 * k0:64 * k1], ps[:, 64:64 + 64 * n]))
        call = S["ans"][gi]
        if call["tg"]:
            g.wait_ge(s.vq, vf())
            trs = []
            for t, m in zip(call["tg"], call["m"]):
                k = S["pos"][t]
                trs.append(_tr(topo, cores[t], m[0], s["rs%d" % P["late"][t][o]], T.respS[:, 64 * k:64 * k + 64],
                               T.land[:, 64 * o:64 * o + 64]))
                loc[0] += m[1]
            g.remote_dma_fused(trs, local_sem=s.loc)


def _server_consts(g, T, v, vf, q, qf):
    A, V = AluOpType, g.vector
    v(V.tensor_scalar(T.Da[:], T.Di[:], 15, None, op0=A.bitwise_and))
    v(V.tensor_scalar(T.Ds[:], T.Di[:, 0:32], 31, None, op0=A.bitwise_and))
    v(V.tensor_scalar(T.pa[:], T.pi[:], 5, None, op0=A.logical_shift_right))
    vf()
    v(V.tensor_scalar(T.Am[:], T.Da[:], 0.0, None, op0=A.is_equal))
    v(V.tensor_scalar(T.S4[:], T.Ds[:], 0.0, None, op0=A.is_equal))
    v(V.tensor_scalar(T.cmO[:], T.pa[:], 2048.0, -63.0, op0=A.mult, op1=A.add))


def _helper_program(g, T, topo, P, r, core):
    s, cores, rq, loc, trs = T.sem, list(T.cores), P["req"][r], [0], []
    V = g.vector
    v, vf = _queue(V, s.vq)
    q, qf = _queue(g, s.gq)
    v(V.memset(T.winT[:, 0:64], 0.0))
    v(V.memset(T.winT[:, 2112:2176], 0.0))
    q(g.iota(T.Di[:], [[1, 128]], 128, -1))
    q(g.iota(T.pi[:], [[0, 1]], 0, 1))
    V.wait_ge(s.gq, qf())
    _server_consts(g, T, v, vf, q, qf)
    g.wait_ge(s.hqs, rq["h_m"][1])
    for o, m in zip(rq["via"], rq["via_m"]):
        S = P["sv"][P["srv"][o][r]]
        k = S["pos"][r]
        trs.append(_tr(topo, P["srv"][o][r], m[0], s["rq%d" % S["cls"][r]], T.hq[:, 8 * o:8 * o + 8],
                       T.reqL[:, 8 * k:8 * k + 8]))
        loc[0] += m[1]
    g.remote_dma_fused(trs, local_sem=s.loc)
    w = 2048 // NQ
    for qd in range(NQ):
        V.wait_ge(s["st%d" % qd], P["stage"][r][qd][1])
        v(V.transpose(T.winT[:, 64 + w * qd:64 + w * qd + w], T.tabS[:, w * qd:w * qd + w]))
    _serve(g, T, topo, P, core, v, vf, [], loc)
    g.wait_ge(s.loc, loc[0])


def rank_program(g, core, T, topo):
    cores = list(T.cores)
    P = _plan(topo, cores)
    me = T.rank_of(core)
    if me is None:
        for r, h in P["helper"].items():
            if h == core:
                _helper_program(g, T, topo, P, r, core)
        return
    A, s = AluOpType, T.sem
    V, PE, AC, SY = g.vector, g.tensor, g.scalar, g.sync
    v, vf = _queue(V, s.vq)
    p, pf = _queue(PE, s.pq)
    q, qf = _queue(g, s.gq)
    CP = ActivationFunctionType.Copy
    loc = [0]
    w = 2048 // NQ
    rp = w // 64

    SY.dma_start(T.ix[:], T.idx[:]).then_inc(s.dix, 16)
    for qd in range(NQ):
        for a in range(4):
            r0 = 1024 * a + 32 * rp * qd
            (SY if a < 2 else AC).dma_start(T.tabS[32 * a:32 * a + 32, w * qd:w * qd + w],
                                            T.tab[r0:r0 + 32 * rp, :]).then_inc(s["dt%d" % qd], 16)

    def stage(qd):
        m = P["stage"][me][qd]
        rid, pid, _ = topo.addr(P["helper"][me])
        g.wait_ge(s["dt%d" % qd], 64)
        g.remote_dma(T.tabS[:, w * qd:w * qd + w], T.tabS[:, w * qd:w * qd + w], s["st%d" % qd], s.loc, pid, rid, m[0])
        loc[0] += m[1]

    v(V.memset(T.onesb[:], 1.0))
    v(V.memset(T.ones64[:], 1.0))
    v(V.memset(T.Hp[:, 0:24], 0.0))
    v(V.memset(T.winT[:, 0:64], 0.0))
    v(V.memset(T.winT[:, 2112:2176], 0.0))
    v(V.memset(T.LT[:, 0:64], 0.0))
    v(V.memset(T.LT[:, 576:640], 0.0))
    v(V.memset(T.Rm[:], 1.0))
    q(g.iota(T.io8[:], [[1, 8]], 0, 0, allow_small_or_imprecise_dtypes=True))
    q(g.iota(T.Di[:], [[1, 128]], 128, -1))
    q(g.iota(T.pi[:], [[0, 1]], 0, 1))
    m1 = qf()
    g.wait_ge(s.vq, vf())
    q(g.affine_select(T.Lb[:], T.onesb[:], [[1, 128]], A.is_ge, 0.0, -1, -1))
    mL = qf()
    q(g.iota(T.ioOZ[:], [[1, 8], [0, 8]], 0, 0, allow_small_or_imprecise_dtypes=True))
    mO = qf()
    q(g.iota(T.io128[:], [[1, 128]], 0, 0, allow_small_or_imprecise_dtypes=True))
    q(g.affine_select(T.mz1[:], T.ones64[:], [[0, 8], [-16, 8]], A.is_ge, 0.0, 0, 1))
    qf()
    q(g.affine_select(T.mOZ[:], T.mz1[:], [[0, 8], [16, 8]], A.is_ge, 0.0, 15, -1))
    m2 = qf()
    if me in P["helper"]:
        for qd in range(EARLY):
            stage(qd)
    V.wait_ge(s.gq, m1)
    for c in range(4):
        v(V.memset(T.Rm[:, 8 * c:8 * c + 1], 0.0))
    _server_consts(g, T, v, vf, q, qf)
    v(V.tensor_scalar(T.cmF[:], T.pa[:], 1024.0, -64.0, op0=A.mult, op1=A.add))

    V.wait_ge(s.dix, 16)
    v(V.tensor_scalar(T.oi[:], T.ix[:], 12, None, op0=A.logical_shift_right))
    v(V.tensor_scalar(T.ti[:], T.ix[:], 7, None, op0=A.bitwise_and))
    v(V.tensor_scalar(T.ki[:], T.ix[:], 3, 31, op0=A.logical_shift_right, op1=A.bitwise_and))
    v(V.tensor_scalar(T.a1[:], T.ix[:], 3840, None, op0=A.bitwise_and))
    vf()
    v(V.tensor_copy(T.of[:], T.oi[:]))
    v(V.tensor_scalar(T.v1[:], T.ti[:], 64.0, None, op0=A.mult))
    v(V.tensor_scalar(T.v2[:], T.a1[:], 2.0, None, op0=A.mult))
    v(V.tensor_scalar(T.kf[:], T.ki[:], 1.0, None, op0=A.add))
    vf()
    v(V.tensor_tensor(T.v3[:], T.v1[:], T.v2[:], A.add))
    for c in range(4):
        v(V.tensor_scalar(T.Hp[:, 24 + 8 * c:32 + 8 * c], T.io8[:], T.of[:, c:c + 1], None, op0=A.is_equal))
    PE.wait_ge(s.vq, vf())
    PE.wait_ge(s.gq, mL)
    p(PE.matmul(T.psS[:, 0:32], T.Lb[:], T.Hp[:, 24:56], True, False))
    for d in (1, 2, 3):
        p(PE.matmul(T.psS[:, 0:32], T.onesb[:], T.Hp[:, 24 - 8 * d:56 - 8 * d], False, d == 3))
    V.wait_ge(s.gq, mO)
    for c in range(4):
        for h, part in enumerate((T.v3, T.kf)):
            v(V.tensor_scalar(T.Rv[:, 128 * c + 64 * h:128 * c + 64 * h + 64], T.ioOZ[:], T.of[:, c:c + 1],
                              part[:, c:c + 1], op0=A.is_equal, op1=A.mult))
    V.wait_ge(s.pq, pf())
    v(V.tensor_tensor(T.tmpS[:], T.Hp[:, 24:56], T.psS[:, 0:32], A.mult))
    vf()
    v(V.tensor_tensor_scan(T.scn[:], T.Rm[:], T.tmpS[:], 0.0, A.mult, A.add))
    vf()
    V.wait_ge(s.gq, m2)
    for c in range(4):
        v(V.tensor_scalar(T.E[:, 128 * c:128 * c + 128], T.io128[:], T.scn[:, 8 * c + 7:8 * c + 8], None, op0=A.is_equal))
    PE.wait_ge(s.vq, vf())
    for c in range(4):
        for h in range(2):
            p(PE.matmul(T.psC[:, 0:64], T.E[:, 128 * c:128 * c + 128], T.Rv[:, 128 * c + 64 * h:128 * c + 64 * h + 64],
                        c == 0 and h == 0, c == 3 and h == 1))
    V.wait_ge(s.pq, pf())
    v(V.tensor_tensor(T.reqS[:], T.psC[:, 0:64], T.mOZ[:], A.mult))
    g.wait_ge(s.vq, vf())
    v(V.tensor_tensor(T.reqL[:, 0:8], T.psC[:, 8 * me:8 * me + 8], T.mOZ[:, 0:8], A.mult))

    rq = P["req"][me]
    if rq["via"]:
        rid, pid, _ = topo.addr(P["helper"][me])
        g.remote_dma(T.hq[:], T.reqS[:], s.hqs, s.loc, pid, rid, rq["h_m"][0])
        loc[0] += rq["h_m"][1]
    trs = []
    for o, m in zip(rq["st"], rq["st_m"]):
        S = P["sv"][P["srv"][o][me]]
        k = S["pos"][me]
        trs.append(_tr(topo, P["srv"][o][me], m[0], s["rq%d" % S["cls"][me]], T.reqS[:, 8 * o:8 * o + 8],
                       T.reqL[:, 8 * k:8 * k + 8]))
        loc[0] += m[1]
    g.remote_dma_fused(trs, local_sem=s.loc)
    if me in P["helper"]:
        for qd in range(EARLY, NQ):
            stage(qd)

    for qd in range(NQ):
        V.wait_ge(s["dt%d" % qd], 64)
    v(V.transpose(T.winT[:, 64:2112], T.tabS[:]))

    def _b2():
        for c in range(4):
            v(V.tensor_scalar(T.B2[:, 8 * c:8 * c + 8], T.mOZ[:, 0:8], T.val2[:, c:c + 1], None, op0=A.mult))
    prep = [
        lambda: (v(V.tensor_copy(T.sli[:], T.scn[:, 7:32:8])), v(V.tensor_scalar(T.o64[:], T.of[:], 64.0, None, op0=A.mult))),
        lambda: (v(V.tensor_scalar(T.hii[:], T.sli[:], 5, None, op0=A.logical_shift_right)),
                 v(V.tensor_tensor(T.w2[:], T.o64[:], T.scn[:, 7:32:8], A.add))),
        lambda: v(V.tensor_scalar(T.hif[:], T.hii[:], 992.0, None, op0=A.mult)),
        lambda: v(V.tensor_tensor(T.val2[:], T.w2[:], T.hif[:], A.add)),
        _b2,
    ]

    _serve(g, T, topo, P, core, v, vf, prep, loc)

    while prep:
        vf()
        prep.pop(0)()
    PE.wait_ge(s.vq, vf())
    p(PE.matmul(T.psF[:, 0:32], T.Am[:], T.B2[:], True, True))
    V.wait_ge(s.pq, pf())
    v(V.tensor_scalar(T.off2[:], T.psF[:, 0:32], T.cmF[:, 0:1], 576.0, op0=A.subtract, op1=A.min))
    vf()

    v(V.transpose(T.LT[:, 64 + 64 * me:128 + 64 * me], T.land[:, 64 * me:64 * me + 64]))
    for lt in range(2):
        if P["rs_tot"][me][lt]:
            V.wait_ge(s["rs%d" % lt], P["rs_tot"][me][lt])
        for o in range(len(cores)):
            if o != me and P["late"][me][o] == lt:
                v(V.transpose(T.LT[:, 64 + 64 * o:128 + 64 * o], T.land[:, 64 * o:64 * o + 64]))
    AC.wait_ge(s.vq, vf())
    banks = [T.psY, T.psS, T.psC, T.psF]
    for c in range(4):
        ofs, fg = T.off2[:, 8 * c:8 * c + 8], s["fg%d" % c]
        V.tensor_copy(T.G2[:, 128 * c:128 * c + 128], T.LT[:, 0:608].indirect(ofs)).then_inc(fg, 1)
        AC.activation(T.G2[:, 512 + 128 * c:512 + 128 * c + 128], T.LT[:, 32:640].indirect(ofs), CP).then_inc(fg, 1)
        PE.wait_ge(fg, 2)
        for h in range(2):
            PE.matmul(banks[c][:, 32 * h:32 * h + 32], T.G2[:, 512 * h + 128 * c:512 * h + 128 * c + 128], T.S4[:],
                      True, True).then_inc(s["fm%d" % c], 1)
    for c in range(4):
        V.wait_ge(s["fm%d" % c], 2)
        V.tensor_copy(T.Ysb[:, 64 * c:64 * c + 64], banks[c][:, 0:64]).then_inc(s["ev%d" % c], 1)
        Q = SY if c % 2 == 0 else AC
        Q.wait_ge(s["ev%d" % c], 1)
        Q.dma_start(T.y[128 * c:128 * c + 128, :], T.Ysb[:, 64 * c:64 * c + 64]).then_inc(s.dy, 16)
    g.wait_ge(s.loc, loc[0])
    g.wait_ge(s.dy, 64)
